import numpy as np, ml_dtypes
CORES = [10,34,74,98]
N = 4
import mx_ref
BF = ml_dtypes.bfloat16
def entries(a):
    return np.ascontiguousarray(a.T).reshape(-1)
def table(e):
    return np.ascontiguousarray(np.reshape(e, (-1, 16)).T).astype(np.int32)
def cols(t, e):
    v = np.concatenate([t.reshape(128, -1, 4), np.zeros((128, 1, 4), BF)], axis=1)
    return np.ascontiguousarray(v[:, e]).reshape(128, -1)
def cut(t, i, w=512):
    return t[:, w * i:w * i + w]
def f(rng, *shape):
    return mx_ref.flush((rng.standard_normal(shape, dtype=np.float32) * np.exp2(rng.integers(-2, 3, shape[:-1] + (1,)))).astype(BF))
def wide(rng, *shape, cols=0):
    v = rng.standard_normal(shape, dtype=np.float32) * np.exp2(rng.integers(-12, 13, shape)).astype(np.float32)
    if cols: v *= np.repeat(np.exp2(rng.integers(-cols, cols + 1, shape[:-2] + (1, shape[-1] // 4))) * (rng.random(shape[:-2] + (1, shape[-1] // 4)) > 0.0625), 4, axis=-1).astype(np.float32)
    return mx_ref.flush(v.astype(BF))
K, B, R, O, CO = 256, 32, 5, 2, 144
def others(d):
    return [s for s in range(N) if s != d]
def numbers_of(a):
    return np.stack([entries(e) for e in a]).reshape(N, R, N, B)
def batch(tab, cs, t, d):
    return np.concatenate([cols(tab[s], cs[s, t, d]) for s in others(d)], axis=1)
def passes(u, new):
    return int(np.sum(mx_ref.matmul(mx_ref.quantize(u), mx_ref.quantize(new))[0] >= 0))
def write(tab, new, keys):
    tab.reshape(128, K, 4)[:, keys] = new.reshape(128, -1, 4)
def level(rng, n, rule, must):
    if rule == "all": return min(n)
    if rule == "none": return max(n) + 1
    if rule == "edge": return max(n)
    v = min(n, key=lambda a: abs(2 * sum(b >= a for b in n) - N))
    low = max([a for a in n if a < v], default=v - 1)
    h = int(rng.integers(low + 1, v + 1))
    return min(h, n[must]) if rule == "chain" else h
def draw_key(rng, at, got, d):
    for _ in range(1000):
        k = int(rng.integers(0, K)); q = divmod(int(at[k]), K)[0]
        if q == d or got[at[k]] or got.reshape(N, K)[q].sum() < CO:
            got[at[k]] = True
            return k
    raise RuntimeError("no key")
def draw_new(rng, at, got, d, q):
    k = np.flatnonzero((at >= q * K) & (at < q * K + K) & ~got[at])
    if len(k) == 0 or got.reshape(N, K)[q].sum() >= CO: return draw_key(rng, at, got, d)
    k = int(rng.choice(k)); got[at[k]] = True
    return k
def game(rng, x, u, rule):
    cs, cd, thr = np.full((N, R, N, B), -1), np.full((N, R, N, B), -1), np.zeros(16, int)
    tab, at = np.array(x, order="C"), np.arange(N * K).reshape(N, K)
    got = np.zeros((N, N * K), bool)
    p, hold, done = rng.permutation(N), rng.permutation(K)[:B], 0
    one, told = int(rng.integers(0, R)), {"all": 0, "none": (N - 1) * B + 1, "chain": (N - 1) * B}
    if rule == "chain":
        got[:, p[0] * K + hold] = True
        u[int(p[(one + 1) % N])] = 0
    for t in range(R):
        a, e = int(p[t % N]), int(p[(t + 1) % N])
        for d in range(N):
            cd[d, t, others(d)] = rng.permutation(K)[:(N - 1) * B].reshape(N - 1, B)
            for s in others(d):
                if rule == "chain" and (s, d) == (a, e): cs[s, t, d] = hold
                elif rule == "all" and d == p[0]: cs[s, t, d] = [draw_new(rng, at[s], got[d], d, int(p[1])) for j in range(B)]
                else: cs[s, t, d] = [draw_key(rng, at[s], got[d], d) for j in range(B)]
        new = [batch(tab, cs, t, d) for d in range(N)]
        src = [np.concatenate([at[s, cs[s, t, d]] for s in others(d)]) for d in range(N)]
        n = [passes(u[d], new[d]) for d in range(N)]
        thr[t] = told[rule] if t == one and rule in told else level(rng, n, rule, e)
        for d in range(N):
            if n[d] >= thr[t]:
                keys = cd[d, t, others(d)].reshape(-1)
                write(tab[d], new[d], keys); at[d, keys] = src[d]; done += 1
        hold = cd[e, t, a]
    return cs, cd, thr, done, int(got[p[0]].reshape(N, K)[p[1]].sum())
def make(rng, rule="half", x=None):
    if x is None: x = f(rng, N, 128, 4 * K)
    u = np.zeros((N, 128, 512), BF); u[:, :, :4] = f(rng, N, 128, 4)
    w = f(rng, N, 128, 512 * R * O)
    for _ in range(50):
        cs, cd, thr, done, most = game(rng, x, u, rule)
        if (rule != "half" or N * R <= 3 * done <= 2 * N * R) and (rule != "all" or most == CO):
            return {"x": x, "u": u, "w": w, "cs": np.stack([table(e.reshape(-1)) for e in cs]), "cd": np.stack([table(e.reshape(-1)) for e in cd]), "thr": np.stack([table(thr) for r in range(N)])}
    raise RuntimeError("no draw")
def setup_inputs(rng):
    return make(rng)
def setup_inputs_all(rng):
    return make(rng, "all")
def setup_inputs_none(rng):
    return make(rng, "none")
def setup_inputs_edge(rng):
    return make(rng, "edge")
def setup_inputs_chain(rng):
    return make(rng, "chain")
def setup_inputs_spread(rng):
    x = np.array(wide(rng, N, 128, 4 * K, cols=6))
    x[np.abs(x.astype(np.float32)) < 2.0 ** -30] = 0
    return make(rng, "half", x)
def check_inputs(d):
    b = []
    for name in ("x", "u", "w"):
        v = np.abs(np.asarray(d[name]).astype(np.float32))
        if not (np.isfinite(v) & ((v == 0) | ((v >= 2.0 ** -30) & (v <= 2.0 ** 30)))).all(): b.append(name + ": a value that isn't finite, or neither zero nor 2**-30 to 2**30 in size")
    cs, cd = numbers_of(d["cs"]), numbers_of(d["cd"])
    for r in range(N):
        for t in range(R):
            if (cs[r, t, r] != -1).any() or (cd[r, t, r] != -1).any(): b.append("a rank's own part isn't -1")
            k, e = cs[r, t, others(r)], cd[r, t, others(r)].reshape(-1)
            if k.min() < 0 or k.max() >= K: b.append("cs")
            if e.min() < 0 or e.max() >= K or len(set(e.tolist())) != len(e): b.append("cd")
        h = entries(d["thr"][r])
        if (h != entries(d["thr"][0])).any(): b.append("thr isn't the same on every rank")
        if h.min() < 0 or h.max() > (N - 1) * B + 1 or (h[R:] != 0).any(): b.append("thr")
    if (np.asarray(d["u"])[:, :, 4:].astype(np.float32) != 0).any(): b.append("u")
    if b: return b
    tab, at = np.array(d["x"], order="C"), np.arange(N * K).reshape(N, K)
    got = np.zeros((N, N * K), bool)
    for t in range(R):
        new = [batch(tab, cs, t, r) for r in range(N)]
        src = [np.concatenate([at[s, cs[s, t, r]] for s in others(r)]) for r in range(N)]
        for r in range(N):
            if passes(d["u"][r], new[r]) >= entries(d["thr"][r])[t]:
                keys = cd[r, t, others(r)].reshape(-1)
                write(tab[r], new[r], keys); at[r, keys] = src[r]; got[r, src[r]] = True
    for r in range(N):
        for q in others(r):
            if got[r].reshape(N, K)[q].sum() > CO: b.append("too many columns of one rank are written on another")
    return b
def reference(x, u, w, cs, cd, thr):
    cs, cd = numbers_of(cs), numbers_of(cd)
    tab = np.array(x, order="C")
    y = np.zeros((N, 128, R * O * K), np.float32)
    for t in range(R):
        new = [batch(tab, cs, t, d) for d in range(N)]
        for d in range(N):
            if passes(u[d], new[d]) >= entries(thr[d])[t]: write(tab[d], new[d], cd[d, t, others(d)].reshape(-1))
            q = mx_ref.quantize(tab[d])
            for o in range(O):
                i = t * O + o
                y[d][:, K * i:K * i + K] = mx_ref.matmul(mx_ref.quantize(cut(w[d], i)), q)
    return {"y": y}

@@ -1,0 +1,318 @@
+from concourse.bass import DstId, RemoteDMATransfer
+from concourse.mybir import dt, AluOpType, ActivationFunctionType
+
+N, K, B, R, O = 4, 256, 32, 5, 2
+NB = (N - 1) * B
+LC = NB // 16
+KC = K // 16
+TW = 2 * K
+GW = 2 * NB
+LW = TW + GW
+NL = KC + LC
+HK = K // 2
+WIN = NB + K
+BW = 4 * LC
+PW = 2 * KC
+
+SCRATCH = {
+    "psc": ("psum", [128, 1024], "float32"),
+    "psy": ("psum", [128, 3072], "float32"),
+    "ci": ("sbuf", [128, 2 * R, 8], "int32"), "cc": ("sbuf", [128, 2 * R, LC], "int32"), "ch": ("sbuf", [128, 2 * R, LC], "int32"),
+    "cp": ("sbuf", [128, 2 * R, LC], "float32"), "bun": ("sbuf", [128, R, BW], "uint16"),
+}
+for _n, _w, _d in (
+        ("xt", 4 * K, "bfloat16"), ("ut", 16, "bfloat16"), ("ur", 512, "bfloat16"), ("zt", 128, "bfloat16"),
+        ("uqc", 128, "float8_e4m3fn_x4"), ("uqs", 128, "uint8"),
+        ("wt", 512 * R * O, "bfloat16"), ("wqc", 128 * R * O, "float8_e4m3fn_x4"), ("wqs", 128 * R * O, "uint8"),
+        ("of0", LC, "uint16"), ("thr1", 16, "int32"), ("thb", 16, "int32"),
+        ("pidx", KC, "int32"), ("p15", KC, "int32"), ("k16", KC, "int32"), ("oddi", 1, "int32"), ("odd16", 1, "float32"),
+        ("pe0", 1, "float32"), ("pe1", 1, "float32"), ("base", 2 * R, "float32"), ("jval", NB, "bfloat16"),
+        ("lb", R * LW, "bfloat16"), ("tb", R * 32 * NL, "bfloat16"), ("lv", R * NL, "float32"), ("lw", PW + 16 * R, "float32"),
+        ("idx", 4 * R, "uint16"), ("offs", 16 * R, "uint16"), ("offt", 16 * R, "uint16"),
+        ("sg", R * NB, "float32"), ("cnt", R, "float32"), ("ysb", R * O * K, "float32")):
+    SCRATCH[_n] = ("sbuf", [128, _w], _d)
+for _t in range(R):
+    SCRATCH["sndc%d" % _t] = ("sbuf", [128, NB], "float8_e4m3fn_x4")
+    SCRATCH["snds%d" % _t] = ("sbuf", [128, NB], "uint8")
+for _t in range(R + 1):
+    SCRATCH["winc%d" % _t] = ("sbuf", [128, WIN], "float8_e4m3fn_x4")
+    SCRATCH["wins%d" % _t] = ("sbuf", [128, WIN], "uint8")
+
+SEMAPHORES = ["xl", "csl", "cdl", "ul", "thl", "iot", "tbc", "ztr", "urr", "uq", "xq", "o0", "vq", "kq", "yl"]
+for _t in range(R):
+    SEMAPHORES += ["%s%d" % (n, _t) for n in ("arr", "snt", "pc", "ps", "tc", "ts", "sco", "act", "ofr", "wl", "wq", "ym", "ev", "ew", "sc", "gt", "fl")]
+SEMAPHORES += ["%s%d%d" % (n, h, o) for n in ("lm", "le") for h in range(2) for o in range(O)] + ["lc0", "lc1", "ls0", "ls1"]
+
+AL = AluOpType
+AF = ActivationFunctionType
+
+
+def rank_program(g, core, T, topo):
+    r = T.rank_of(core)
+    if r is None:
+        return
+    others = [s for s in range(N) if s != r]
+    V, S, X, Y = g.vector, g.scalar, g.tensor, g.sync
+    total = {}
+    waited = {}
+
+    def up(call, name, n=1):
+        call.then_inc(T.sem[name], n)
+        total[name] = total.get(name, 0) + n
+
+    def wait(q, name):
+        q.wait_ge(T.sem[name], total[name])
+        waited[name] = total[name]
+
+    def v(call, name="vq"):
+        up(call, name)
+
+    def vw():
+        wait(V, "vq")
+
+    def load_w(t):
+        up(Y.dma_start(T.wt[:, 1024 * t:1024 * t + 1024], T.w[:, 1024 * t:1024 * t + 1024]), "wl%d" % t, 16)
+
+    def store_y(t):
+        wait(Y, "ev%d" % t)
+        up(Y.dma_start(T.y[:, O * K * t:O * K * (t + 1)], T.ysb[:, O * K * t:O * K * (t + 1)]), "yl", 16)
+
+    BETWEEN = ((("w", 2),), (("w", 3),), (("w", 4), ("y", 0)), (("y", 1),), (("y", 2), ("y", 3)))
+
+    def between(t):
+        wait(Y, "snt%d" % t)
+        for kind, i in BETWEEN[t]:
+            (load_w if kind == "w" else store_y)(i)
+
+    up(Y.dma_start(T.ci[0:16, 0:R, :], T.cs[:, :]), "csl", 16)
+    up(S.dma_start(T.ci[16:32, 0:R, :], T.cs[:, :]), "csl", 16)
+    up(Y.dma_start(T.xt[:, :], T.x[:, :]), "xl", 16)
+    up(S.dma_start(T.ci[0:16, R:2 * R, :], T.cd[:, :]), "cdl", 16)
+    up(S.dma_start(T.ci[16:32, R:2 * R, :], T.cd[:, :]), "cdl", 16)
+    up(Y.dma_start(T.ut[:, :], T.u[:, 0:16]), "ul", 16)
+    up(Y.dma_start(T.thr1[0:1, :], T.thr[:, :]), "thl", 16)
+    load_w(0)
+    load_w(1)
+
+    up(g.iota(T.pidx[:, :], [[0, KC]], 0, 1), "iot")
+    up(g.iota(T.k16[:, :], [[16, KC]], NB, 0), "iot")
+    up(g.iota(T.jval[:, :], [[1, NB]], 0, 0, allow_small_or_imprecise_dtypes=True), "iot")
+
+    v(V.memset(T.lb[:, 0:TW], 512.0), "fl0")
+    v(V.memset(T.zt[:, :], 0.0), "ztr")
+    wait(V, "iot")
+    v(V.tensor_scalar(T.p15[:, :], T.pidx[:, :], 15, None, AL.bitwise_and))
+    v(V.tensor_scalar(T.oddi[:, :], T.pidx[:, 0:1], 16, None, AL.bitwise_and))
+    vw()
+    v(V.tensor_tensor(T.lw[:, 0:PW:2], T.p15[:, :], T.k16[:, :], AL.add))
+    v(V.tensor_copy(T.odd16[:, :], T.oddi[:, :]))
+    v(V.tensor_scalar(T.pe0[:, :], T.p15[:, 0:1], 1024.0, 256.0 + NB + 1, AL.mult, AL.add))
+
+    runs = []
+    if r > 0:
+        runs.append((0, 0, 2 * r))
+    if r < N - 1:
+        runs.append((2 * r + 2, 2 * r, LC - 2 * r))
+    q0 = slice(0, 32)
+
+    wait(V, "csl")
+    for a, b, n in runs:
+        v(V.tensor_copy(T.of0[q0, b:b + n], T.ci[q0, 0, a:a + n]), "o0")
+    wait(V, "o0")
+    for k in (32, 64, 96):
+        v(V.tensor_copy(T.of0[k:k + 32, :], T.of0[q0, :]), "o0")
+    wait(V, "xl")
+    v(V.quantize_mx(T.winc0[:, NB:WIN], T.wins0[:, NB:WIN], T.xt[:, :]), "xq")
+    wait(V, "o0")
+    wait(V, "xq")
+    v(V.tensor_copy(T.sndc0[:, :].bitcast(dt.uint32), T.winc0[:, NB:WIN].bitcast(dt.uint32).indirect(T.of0[:, :])), "pc0")
+    wait(S, "o0")
+    wait(S, "xq")
+    up(S.activation(T.snds0[:, :], T.wins0[:, NB:WIN].indirect(T.of0[:, :]), AF.Copy), "ps0")
+
+    def piece(kind, t, b, first, n):
+        d = others[b]
+        to = T.cores[d]
+        rid, pid, _ = topo.addr(to)
+        at = B * (r if r < d else r - 1)
+        src = T["snd%s%d" % (kind, t)][:, B * b:B * b + B]
+        dst = T["win%s%d" % (kind, t)][:, at:at + B]
+        if kind == "c":
+            src, dst = src.bitcast(dt.uint8), dst.bitcast(dt.uint8)
+        return RemoteDMATransfer(dst_ids=[DstId(rid=rid, pnc=pid)], dma_engine_mask=sum(1 << e for e in topo.engines(core, to)[first:first + n]),
+                                 remote_sem=T.sem["arr%d" % t], srcs=[src], dsts=[dst])
+
+    PLAN = (("c", ((0, 0, 4), (1, 4, 2), (2, 6, 2))), ("s", ((0, 0, 2), (1, 2, 2), (2, 4, 4))))
+
+    def send(t):
+        n = 0
+        for kind, tr in PLAN:
+            wait(g, "p%s%d" % (kind, t))
+            g.remote_dma_fused([piece(kind, t, *p) for p in tr], local_sem=T.sem["snt%d" % t])
+            n += sum(p[2] for p in tr)
+        total["snt%d" % t] = n
+        total["arr%d" % t] = sum(p[2] for s in others for _, tr in PLAN for p in tr if [d for d in range(N) if d != s][p[0]] == r)
+
+    def fill(t):
+        up(g.iota(T.lb[:, LW * t:LW * t + TW], [[0, TW]], 512, 0, allow_small_or_imprecise_dtypes=True), "fl%d" % t)
+
+    send(0)
+
+    wait(g, "thl")
+    up(g.partition_broadcast(T.thb[:, :], T.thr1[0:1, :], 128), "tbc")
+    fill(1)
+
+    wait(S, "ul")
+    wait(S, "ztr")
+    for i in range(4):
+        up(S.activation(T.ur[:, i:512:4], T.zt[:, :], AF.Identity, bias=T.ut[:, i:i + 1]), "urr")
+
+    wait(V, "cdl")
+    for a, b, n in runs:
+        v(V.tensor_copy(T.cc[q0, :, b:b + n], T.ci[q0, :, a:a + n]))
+    vw()
+    v(V.tensor_scalar(T.ch[q0, :, :], T.cc[q0, :, :], 240, None, AL.bitwise_and))
+    v(V.tensor_copy(T.bun[q0, :, 3 * LC:BW], T.cc[q0, 0:R, :]))
+    vw()
+    v(V.tensor_tensor(T.cp[q0, :, :], T.cc[q0, :, :], T.ch[q0, :, :], AL.add))
+    vw()
+    v(V.tensor_scalar(T.bun[q0, :, 0:LC], T.cp[q0, R:2 * R, :], T.odd16[q0, 0:1], None, AL.add))
+    for i in range(2):
+        v(V.tensor_scalar(T.bun[q0, :, LC + i:3 * LC:2], T.cp[q0, 0:R, :], T.odd16[q0, 0:1], None, AL.add))
+    vw()
+    for k in (32, 64, 96):
+        v(V.tensor_copy(T.bun[k:k + 32, :, :], T.bun[q0, :, :]))
+
+    def lists_begin(t):
+        z = LW * t
+        wait(V, "fl%d" % t)
+        vw()
+        v(V.tensor_copy(T.lb[:, z:z + TW].indirect(T.bun[:, t, 0:LC]), T.jval[:, :]), "sc%d" % t)
+        if t + 1 < R:
+            p = PW + 16 * t
+            v(V.tensor_scalar(T.lw[:, p:p + 2 * LC:2], T.bun[:, t + 1, 3 * LC:BW], float(NB), None, AL.add))
+            wait(S, "sc%d" % t)
+            up(S.activation(T.lb[:, z + TW:z + LW], T.lb[:, z:z + TW].indirect(T.bun[:, t + 1, LC:3 * LC]), AF.Copy), "gt%d" % t)
+
+    def lists_end(t):
+        z, q, y = LW * t, NL * t, 32 * NL * t
+        n = NL if t + 1 < R else KC
+        wait(V, "sc%d" % t)
+        if t + 1 < R:
+            wait(V, "gt%d" % t)
+        v(V.transpose(T.tb[:, y:y + 32 * n], T.lb[:, z:z + 32 * n]))
+        vw()
+        v(V.tensor_tensor(T.lv[:, q:q + n], T.tb[:, y:y + 32 * n:32], T.tb[:, y + 16:y + 32 * n:32], AL.min))
+        vw()
+        v(V.tensor_tensor(T.lw[:, 1:PW:2], T.lv[:, q:q + KC], T.lw[:, 0:PW:2], AL.min))
+        if t + 1 < R:
+            p = PW + 16 * t
+            v(V.tensor_tensor(T.lw[:, p + 1:p + 2 * LC:2], T.lv[:, q + KC:q + NL], T.lw[:, p:p + 2 * LC:2], AL.min))
+
+    lists_begin(0)
+    v(V.tensor_scalar(T.pe1[:, :], T.pe0[:, :], 1024.0 * (LC - 1) + 256.0 + NB + 1, None, AL.min))
+    wait(V, "tbc")
+    vw()
+    v(V.tensor_scalar(T.base[:, 0:R], T.thb[:, 0:R], -2.0, T.pe0[:, 0:1], AL.mult, AL.add))
+    v(V.tensor_scalar(T.base[:, R:2 * R], T.thb[:, 0:R], -2.0, T.pe1[:, 0:1], AL.mult, AL.add))
+    wait(V, "urr")
+    v(V.quantize_mx(T.uqc[:, :], T.uqs[:, :], T.ur[:, :]), "uq")
+    lists_end(0)
+
+    def quantize_w(t):
+        wait(V, "wl%d" % t)
+        for i in (2 * t, 2 * t + 1):
+            v(V.quantize_mx(T.wqc[:, 128 * i:128 * i + 128], T.wqs[:, 128 * i:128 * i + 128], T.wt[:, 512 * i:512 * i + 512]), "wq%d" % t)
+
+    def product(i, bank, cols, win, name):
+        p = 512 * bank
+        a, b = NB + cols[0], NB + cols[1]
+        up(X.matmul_mx(T.psy[:, p:p + b - a], T.wqc[:, 128 * i:128 * i + 128], T.wqs[:, 128 * i:128 * i + 128], win[0][:, a:b], win[1][:, a:b], True, True), name)
+
+    between(0)
+
+    for t in range(R):
+        last = t + 1 == R
+        wc, ws = T["winc%d" % t], T["wins%d" % t]
+        nc, ns = T["winc%d" % (t + 1)], T["wins%d" % (t + 1)]
+        if t == 0:
+            wait(X, "uq")
+            wait(X, "xq")
+        wait(X, "arr%d" % t)
+        bank = 512 * (t % 2)
+        up(X.matmul_mx(T.psc[:, bank:bank + 128], T.uqc[:, :], T.uqs[:, :], wc[:, 0:128], ws[:, 0:128], True, True), "sco%d" % t)
+        wait(S, "sco%d" % t)
+        up(S.activation(T.sg[:, NB * t:NB * t + NB], T.psc[:, bank:bank + NB], AF.Sign, bias=-1e-30, scale=-1.0, accum_out=T.cnt[:, t:t + 1]), "act%d" % t)
+        vw()
+        wait(V, "act%d" % t)
+        v(V.tensor_scalar(T.idx[:, 4 * t:4 * t + 4:2], T.base[:, t:2 * R:R], T.cnt[:, t:t + 1], 1.0 / 512, AL.subtract, AL.mult))
+        vw()
+        if not last:
+            v(V.tensor_copy(T.offs[:, 16 * t:16 * t + 16], T.lw[:, PW + 16 * t:PW + 16 * t + 2 * LC].indirect(T.idx[:, 4 * t + 2:4 * t + 3])), "ofr%d" % t)
+            wait(V, "ofr%d" % t)
+            oc = T.offs[:, 16 * t:16 * t + LC]
+            v(V.tensor_copy(T["sndc%d" % (t + 1)][:, :].bitcast(dt.uint32), wc[:, :].bitcast(dt.uint32).indirect(oc)), "pc%d" % (t + 1))
+            wait(S, "ofr%d" % t)
+            up(S.activation(T["snds%d" % (t + 1)][:, :], ws[:, :].indirect(oc), AF.Copy), "ps%d" % (t + 1))
+            send(t + 1)
+            if t + 2 < R:
+                fill(t + 2)
+        v(V.tensor_copy(T.offt[:, 16 * t:16 * t + 16], T.lw[:, 0:PW].indirect(T.idx[:, 4 * t:4 * t + 1])), "ew%d" % t)
+        wait(V, "ew%d" % t)
+        wait(S, "ew%d" % t)
+        if last:
+            break
+        oc = T.offt[:, 16 * t:16 * t + KC]
+        v(V.tensor_copy(nc[:, NB:WIN].bitcast(dt.uint32), wc[:, :].bitcast(dt.uint32).indirect(oc)), "tc%d" % t)
+        up(S.activation(ns[:, NB:WIN], ws[:, :].indirect(oc), AF.Copy), "ts%d" % t)
+        lists_begin(t + 1)
+        quantize_w(t)
+        if t == R - 2:
+            quantize_w(t + 1)
+        lists_end(t + 1)
+        wait(X, "tc%d" % t)
+        wait(X, "ts%d" % t)
+        wait(X, "wq%d" % t)
+        if t >= 3:
+            wait(X, "ev%d" % (t - 3))
+        for o in range(O):
+            i = O * t + o
+            product(i, i % 6, (0, K), (nc, ns), "ym%d" % t)
+        wait(S, "ym%d" % t)
+        for o in range(O):
+            i = O * t + o
+            up(S.activation(T.ysb[:, K * i:K * i + K], T.psy[:, 512 * (i % 6):512 * (i % 6) + K], AF.Copy), "ev%d" % t)
+        between(t + 1)
+
+    t = R - 1
+    for h in range(2):
+        oc = T.offt[:, 16 * t + KC // 2 * h:16 * t + KC // 2 * (h + 1)]
+        at = slice(NB + HK * h, NB + HK * h + HK)
+        v(V.tensor_copy(nc[:, at].bitcast(dt.uint32), wc[:, :].bitcast(dt.uint32).indirect(oc)), "lc%d" % h)
+        up(S.activation(ns[:, at], ws[:, :].indirect(oc), AF.Copy), "ls%d" % h)
+    wait(X, "wq%d" % t)
+    wait(X, "ev1")
+    wait(X, "ev2")
+    for h in range(2):
+        wait(X, "lc%d" % h)
+        wait(X, "ls%d" % h)
+        for o in range(O):
+            product(O * t + o, 2 + 2 * h + o, (HK * h, HK * h + HK), (nc, ns), "lm%d%d" % (h, o))
+    for h in range(2):
+        for o in range(O):
+            p = 512 * (2 + 2 * h + o)
+            c = K * (O * t + o) + HK * h
+            wait(V if o else S, "lm%d%d" % (h, o))
+            if o:
+                v(V.tensor_copy(T.ysb[:, c:c + HK], T.psy[:, p:p + HK]), "le%d%d" % (h, o))
+            else:
+                up(S.activation(T.ysb[:, c:c + HK], T.psy[:, p:p + HK], AF.Copy), "le%d%d" % (h, o))
+    for h in range(2):
+        for o in range(O):
+            c = K * (O * t + o) + HK * h
+            on = S if h == 1 and o == 0 else Y
+            wait(on, "le%d%d" % (h, o))
+            up(on.dma_start(T.y[:, c:c + HK], T.ysb[:, c:c + HK]), "kq" if on is S else "yl", 16)
+    for name in total:
+        if waited.get(name, 0) < total[name]:
+            wait(Y, name)

@@ -8,40 +8,51 @@ KC = K // 16
 TW = 2 * K
 GW = 2 * NB
 LW = TW + GW
-NL = KC + LC
+LU = LW + B
 HK = K // 2
 WIN = NB + K
-BW = 4 * LC
+BG, BK = LC, 3 * LC + 2
+BW = BK + LC
 PW = 2 * KC
+PE = PW + 2 * LC
+PA = PE + 4
+LESS = 128
 
 SCRATCH = {
     "psc": ("psum", [128, 1024], "float32"),
     "psy": ("psum", [128, 3072], "float32"),
     "ci": ("sbuf", [128, 2 * R, 8], "int32"), "cc": ("sbuf", [128, 2 * R, LC], "int32"), "ch": ("sbuf", [128, 2 * R, LC], "int32"),
-    "cp": ("sbuf", [128, 2 * R, LC], "float32"), "bun": ("sbuf", [128, R, BW], "uint16"),
+    "cp": ("sbuf", [128, 2 * R, LC], "float32"), "bun": ("sbuf", [128, R, BW], "uint16"), "lw": ("sbuf", [128, R - 1, PA], "float32"),
+    "lz": ("sbuf", [128, 4, 32], "bfloat16"), "tz": ("sbuf", [128, 4, 32], "bfloat16"),
 }
 for _n, _w, _d in (
         ("xt", 4 * K, "bfloat16"), ("ut", 16, "bfloat16"), ("ur", 512, "bfloat16"), ("zt", 128, "bfloat16"),
         ("uqc", 128, "float8_e4m3fn_x4"), ("uqs", 128, "uint8"),
         ("wt", 512 * R * O, "bfloat16"), ("wqc", 128 * R * O, "float8_e4m3fn_x4"), ("wqs", 128 * R * O, "uint8"),
-        ("of0", LC, "uint16"), ("thr1", 16, "int32"), ("thb", 16, "int32"),
-        ("pidx", KC, "int32"), ("p15", KC, "int32"), ("k16", KC, "int32"), ("oddi", 1, "int32"), ("odd16", 1, "float32"),
-        ("pe0", 1, "float32"), ("pe1", 1, "float32"), ("base", 2 * R, "float32"), ("jval", NB, "bfloat16"),
-        ("lb", R * LW, "bfloat16"), ("tb", R * 32 * NL, "bfloat16"), ("lv", R * NL, "float32"), ("lw", PW + 16 * R, "float32"),
-        ("idx", 4 * R, "uint16"), ("offs", 16 * R, "uint16"), ("offt", 16 * R, "uint16"),
-        ("sg", R * NB, "float32"), ("cnt", R, "float32"), ("ysb", R * O * K, "float32")):
+        ("of0", 8, "uint16"), ("thr1", 16, "int32"), ("thb", 16, "int32"),
+        ("pidx", KC, "int32"), ("p15", KC, "int32"), ("k16", KC, "int32"), ("oddi", 1, "int32"),
+        ("odd16", 1, "float32"), ("even16", 1, "float32"),
+        ("pe0", 1, "float32"), ("pe1", 1, "float32"), ("base", 3 * R, "float32"), ("jval", NB, "bfloat16"),
+        ("la", LU, "bfloat16"), ("ta", LW, "bfloat16"), ("lb", TW, "bfloat16"), ("tb", TW, "bfloat16"), ("lq", PA, "float32"),
+        ("idx", 4 * R, "uint16"), ("offt", 16 * R, "uint16"), ("offa", 4 * R, "uint16"),
+        ("sg", R * NB, "float32"), ("cnt", R, "float32"), ("ysb", R * O * K, "float32"),
+        ("yw", WIN, "float32"), ("endc", K, "float8_e4m3fn_x4"), ("ends", K, "uint8")):
     SCRATCH[_n] = ("sbuf", [128, _w], _d)
 for _t in range(R):
-    SCRATCH["sndc%d" % _t] = ("sbuf", [128, NB], "float8_e4m3fn_x4")
-    SCRATCH["snds%d" % _t] = ("sbuf", [128, NB], "uint8")
-for _t in range(R + 1):
+    SCRATCH["sndc%d" % _t] = ("sbuf", [128, N * B], "float8_e4m3fn_x4")
+    SCRATCH["snds%d" % _t] = ("sbuf", [128, N * B], "uint8")
+    SCRATCH["offs%d" % _t] = ("sbuf", [128, 16], "uint16")
+    SCRATCH["twoc%d" % _t] = ("sbuf", [128, 2 * B], "float8_e4m3fn_x4")
+    SCRATCH["twos%d" % _t] = ("sbuf", [128, 2 * B], "uint8")
     SCRATCH["winc%d" % _t] = ("sbuf", [128, WIN], "float8_e4m3fn_x4")
     SCRATCH["wins%d" % _t] = ("sbuf", [128, WIN], "uint8")
 
-SEMAPHORES = ["xl", "csl", "cdl", "ul", "thl", "iot", "tbc", "ztr", "urr", "uq", "xq", "o0", "vq", "kq", "yl"]
+SEMAPHORES = ["xl", "csl", "cdl", "ul", "thl", "iot", "iok", "ioj", "fla", "flb", "tbc", "ztr", "urr", "uq", "xq", "o0", "vq", "kq", "yl",
+              "sca", "gta", "lqr", "lqa", "lzr", "om", "oe", "nm", "ne", "lp"]
 for _t in range(R):
-    SEMAPHORES += ["%s%d" % (n, _t) for n in ("arr", "snt", "pc", "ps", "tc", "ts", "sco", "act", "ofr", "wl", "wq", "ym", "ev", "ew", "sc", "gt", "fl")]
-SEMAPHORES += ["%s%d%d" % (n, h, o) for n in ("lm", "le") for h in range(2) for o in range(O)] + ["lc0", "lc1", "ls0", "ls1"]
+    SEMAPHORES += ["%s%d" % (n, _t) for n in ("arr", "snt", "pa", "pb", "ps", "two", "ix", "oa", "tc", "ts", "sco", "act", "ofr",
+                                              "wl", "wq", "ym", "yn", "ev", "ew", "lw")]
+SEMAPHORES += ["%s%d" % (n, o) for n in ("lm", "le", "lc") for o in range(2)]
 
 AL = AluOpType
 AF = ActivationFunctionType
@@ -70,6 +81,10 @@ def rank_program(g, core, T, topo):
     def vw():
         wait(V, "vq")
 
+    def both(name):
+        wait(V, name)
+        wait(S, name)
+
     def load_w(t):
         up(Y.dma_start(T.wt[:, 1024 * t:1024 * t + 1024], T.w[:, 1024 * t:1024 * t + 1024]), "wl%d" % t, 16)
 
@@ -77,7 +92,7 @@ def rank_program(g, core, T, topo):
         wait(Y, "ev%d" % t)
         up(Y.dma_start(T.y[:, O * K * t:O * K * (t + 1)], T.ysb[:, O * K * t:O * K * (t + 1)]), "yl", 16)
 
-    BETWEEN = ((("w", 2),), (("w", 3),), (("w", 4), ("y", 0)), (("y", 1),), (("y", 2), ("y", 3)))
+    BETWEEN = ((("w", 1), ("w", 2)), (("w", 3), ("y", 0)), (("w", 4), ("y", 1)), (("y", 2),), (("y", 3),))
 
     def between(t):
         wait(Y, "snt%d" % t)
@@ -92,227 +107,293 @@ def rank_program(g, core, T, topo):
     up(Y.dma_start(T.ut[:, :], T.u[:, 0:16]), "ul", 16)
     up(Y.dma_start(T.thr1[0:1, :], T.thr[:, :]), "thl", 16)
     load_w(0)
-    load_w(1)
+
+    def fill(table, n, name):
+        up(g.iota(table[:, 0:32 * n], [[16, n], [0, 2], [1, 16]], NB - LESS, 0, allow_small_or_imprecise_dtypes=True), name)
 
     up(g.iota(T.pidx[:, :], [[0, KC]], 0, 1), "iot")
-    up(g.iota(T.k16[:, :], [[16, KC]], NB, 0), "iot")
-    up(g.iota(T.jval[:, :], [[1, NB]], 0, 0, allow_small_or_imprecise_dtypes=True), "iot")
+    up(g.iota(T.k16[:, :], [[16, KC]], NB - LESS, 0), "iok")
+    fill(T.la, KC // 4, "fla")
+    up(g.iota(T.jval[:, :], [[1, NB]], -LESS, 0, allow_small_or_imprecise_dtypes=True), "ioj")
 
-    v(V.memset(T.lb[:, 0:TW], 512.0), "fl0")
     v(V.memset(T.zt[:, :], 0.0), "ztr")
     wait(V, "iot")
     v(V.tensor_scalar(T.p15[:, :], T.pidx[:, :], 15, None, AL.bitwise_and))
     v(V.tensor_scalar(T.oddi[:, :], T.pidx[:, 0:1], 16, None, AL.bitwise_and))
     vw()
-    v(V.tensor_tensor(T.lw[:, 0:PW:2], T.p15[:, :], T.k16[:, :], AL.add))
-    v(V.tensor_copy(T.odd16[:, :], T.oddi[:, :]))
     v(V.tensor_scalar(T.pe0[:, :], T.p15[:, 0:1], 1024.0, 256.0 + NB + 1, AL.mult, AL.add))
+    v(V.tensor_copy(T.odd16[:, :], T.oddi[:, :]))
+    v(V.tensor_scalar(T.even16[:, :], T.oddi[:, :], -1.0, 16.0, AL.mult, AL.add))
+    wait(V, "iok")
+    v(V.tensor_tensor(T.lq[:, 0:PW:2], T.p15[:, :], T.k16[:, :], AL.add))
+    vw()
+    v(V.tensor_scalar(T.pe1[:, :], T.pe0[:, :], 1024.0 * (LC - 1) + 256.0 + NB + 1, None, AL.min))
+
+    def roles(s):
+        rest = [d for d in range(N) if d != s]
+        return sorted(rest, key=lambda d: (topo.same_plane(topo.chip(T.cores[s]), topo.chip(T.cores[d])), d == rest[1], abs(d - s)))
 
     runs = []
     if r > 0:
         runs.append((0, 0, 2 * r))
     if r < N - 1:
         runs.append((2 * r + 2, 2 * r, LC - 2 * r))
-    q0 = slice(0, 32)
+    q = [slice(32 * k, 32 * k + 32) for k in range(4)]
 
     wait(V, "csl")
-    for a, b, n in runs:
-        v(V.tensor_copy(T.of0[q0, b:b + n], T.ci[q0, 0, a:a + n]), "o0")
-    wait(V, "o0")
-    for k in (32, 64, 96):
-        v(V.tensor_copy(T.of0[k:k + 32, :], T.of0[q0, :]), "o0")
+    for k in range(4):
+        v(V.tensor_copy(T.of0[q[k], :], T.ci[q[0], 0, :]), "o0")
     wait(V, "xl")
     v(V.quantize_mx(T.winc0[:, NB:WIN], T.wins0[:, NB:WIN], T.xt[:, :]), "xq")
-    wait(V, "o0")
-    wait(V, "xq")
-    v(V.tensor_copy(T.sndc0[:, :].bitcast(dt.uint32), T.winc0[:, NB:WIN].bitcast(dt.uint32).indirect(T.of0[:, :])), "pc0")
-    wait(S, "o0")
-    wait(S, "xq")
-    up(S.activation(T.snds0[:, :], T.wins0[:, NB:WIN].indirect(T.of0[:, :]), AF.Copy), "ps0")
 
-    def piece(kind, t, b, first, n):
-        d = others[b]
-        to = T.cores[d]
-        rid, pid, _ = topo.addr(to)
+    def block(t, role):
+        d = roles(r)[role]
+        return d if t == 0 else others.index(d)
+
+    def pick(codes, scales, wc, ws, oc, names):
+        v(V.tensor_copy(codes.bitcast(dt.uint32), wc.bitcast(dt.uint32).indirect(oc)), names[0])
+        up(S.activation(scales, ws.indirect(oc), AF.Copy), names[1])
+
+    def pick_hop(t, first, wc, ws, oc):
+        b, n = (block(t, 0), 1) if first else (min(block(t, 1), block(t, 2)), 2)
+        at = slice(B * b, B * (b + n))
+        pick(T["sndc%d" % t][:, at], T["snds%d" % t][:, at], wc, ws, oc(2 * b, 2 * (b + n)), ("p%s%d" % ("a" if first else "b", t), "ps%d" % t))
+
+    both("o0")
+    both("xq")
+    for first in (True, False):
+        pick_hop(0, first, T.winc0[:, NB:WIN], T.wins0[:, NB:WIN], lambda a, b: T.of0[:, a:b])
+
+    PLAN = (("a", "c", ((0, 0, 1),)), ("b", "c", ((1, 0, 2), (2, 1, 2))), ("s", "s", ((0, 0, 2), (1, 1, 2))), ("s", "s", ((2, 0, 1),)))
+
+    def engines(s, role, first, step):
+        return topo.engines(T.cores[s], T.cores[roles(s)[role]])[first::step]
+
+    def piece(kind, t, role, first, step):
+        d = roles(r)[role]
+        rid, pid, _ = topo.addr(T.cores[d])
+        b = block(t, role)
         at = B * (r if r < d else r - 1)
         src = T["snd%s%d" % (kind, t)][:, B * b:B * b + B]
         dst = T["win%s%d" % (kind, t)][:, at:at + B]
         if kind == "c":
             src, dst = src.bitcast(dt.uint8), dst.bitcast(dt.uint8)
-        return RemoteDMATransfer(dst_ids=[DstId(rid=rid, pnc=pid)], dma_engine_mask=sum(1 << e for e in topo.engines(core, to)[first:first + n]),
+        return RemoteDMATransfer(dst_ids=[DstId(rid=rid, pnc=pid)], dma_engine_mask=sum(1 << e for e in engines(r, role, first, step)),
                                  remote_sem=T.sem["arr%d" % t], srcs=[src], dsts=[dst])
-
-    PLAN = (("c", ((0, 0, 4), (1, 4, 2), (2, 6, 2))), ("s", ((0, 0, 2), (1, 2, 2), (2, 4, 4))))
 
     def send(t):
         n = 0
-        for kind, tr in PLAN:
-            wait(g, "p%s%d" % (kind, t))
+        for i, (ready, kind, tr) in enumerate(PLAN):
+            if i == 0 or PLAN[i - 1][0] != ready:
+                wait(g, "p%s%d" % (ready, t))
             g.remote_dma_fused([piece(kind, t, *p) for p in tr], local_sem=T.sem["snt%d" % t])
-            n += sum(p[2] for p in tr)
+            n += sum(len(engines(r, *p)) for p in tr)
         total["snt%d" % t] = n
-        total["arr%d" % t] = sum(p[2] for s in others for _, tr in PLAN for p in tr if [d for d in range(N) if d != s][p[0]] == r)
-
-    def fill(t):
-        up(g.iota(T.lb[:, LW * t:LW * t + TW], [[0, TW]], 512, 0, allow_small_or_imprecise_dtypes=True), "fl%d" % t)
+        total["arr%d" % t] = sum(len(engines(s, *p)) for s in others for _, _, tr in PLAN for p in tr if roles(s)[p[0]] == r)
 
     send(0)
 
     wait(g, "thl")
     up(g.partition_broadcast(T.thb[:, :], T.thr1[0:1, :], 128), "tbc")
-    fill(1)
+    fill(T.lb, KC, "flb")
+
+    for n in (TW // 4, TW // 2):
+        wait(S, "fla")
+        up(S.activation(T.la[:, n:2 * n], T.la[:, 0:n], AF.Identity, bias=float(n // 2)), "fla")
 
     wait(S, "ul")
     wait(S, "ztr")
     for i in range(4):
         up(S.activation(T.ur[:, i:512:4], T.zt[:, :], AF.Identity, bias=T.ut[:, i:i + 1]), "urr")
 
+    q0, there, here = q[0], slice(1, R), slice(R, 2 * R)
+    ba = block(1, 0)
     wait(V, "cdl")
     for a, b, n in runs:
-        v(V.tensor_copy(T.cc[q0, :, b:b + n], T.ci[q0, :, a:a + n]))
+        v(V.tensor_copy(T.cc[q0, 1:, b:b + n], T.ci[q0, 1:, a:a + n]))
     vw()
-    v(V.tensor_scalar(T.ch[q0, :, :], T.cc[q0, :, :], 240, None, AL.bitwise_and))
-    v(V.tensor_copy(T.bun[q0, :, 3 * LC:BW], T.cc[q0, 0:R, :]))
+    v(V.tensor_scalar(T.ch[q0, 1:, :], T.cc[q0, 1:, :], 240, None, AL.bitwise_and))
+    v(V.tensor_copy(T.bun[q0, 0:R - 1, BK:BW], T.cc[q0, there, :]))
     vw()
-    v(V.tensor_tensor(T.cp[q0, :, :], T.cc[q0, :, :], T.ch[q0, :, :], AL.add))
+    v(V.tensor_tensor(T.cp[q0, 1:, :], T.cc[q0, 1:, :], T.ch[q0, 1:, :], AL.add))
     vw()
-    v(V.tensor_scalar(T.bun[q0, :, 0:LC], T.cp[q0, R:2 * R, :], T.odd16[q0, 0:1], None, AL.add))
+    v(V.tensor_scalar(T.bun[q0, :, 0:LC], T.cp[q0, here, :], T.odd16[q0, 0:1], None, AL.add))
     for i in range(2):
-        v(V.tensor_scalar(T.bun[q0, :, LC + i:3 * LC:2], T.cp[q0, 0:R, :], T.odd16[q0, 0:1], None, AL.add))
+        v(V.tensor_scalar(T.bun[q0, 0:R - 1, BG + i:BK - 2:2], T.cp[q0, there, :], T.odd16[q0, 0:1], None, AL.add))
+    v(V.tensor_scalar(T.bun[q0, 0:R - 1, BK - 2:BK], T.cp[q0, there, 2 * ba:2 * ba + 2], T.even16[q0, 0:1], None, AL.add))
     vw()
-    for k in (32, 64, 96):
-        v(V.tensor_copy(T.bun[k:k + 32, :, :], T.bun[q0, :, :]))
+    for k in range(1, 4):
+        v(V.tensor_copy(T.bun[q[k], 0, :], T.bun[q0, k, :]))
 
-    def lists_begin(t):
-        z = LW * t
-        wait(V, "fl%d" % t)
-        vw()
-        v(V.tensor_copy(T.lb[:, z:z + TW].indirect(T.bun[:, t, 0:LC]), T.jval[:, :]), "sc%d" % t)
-        if t + 1 < R:
-            p = PW + 16 * t
-            v(V.tensor_scalar(T.lw[:, p:p + 2 * LC:2], T.bun[:, t + 1, 3 * LC:BW], float(NB), None, AL.add))
-            wait(S, "sc%d" % t)
-            up(S.activation(T.lb[:, z + TW:z + LW], T.lb[:, z:z + TW].indirect(T.bun[:, t + 1, LC:3 * LC]), AF.Copy), "gt%d" % t)
-
-    def lists_end(t):
-        z, q, y = LW * t, NL * t, 32 * NL * t
-        n = NL if t + 1 < R else KC
-        wait(V, "sc%d" % t)
-        if t + 1 < R:
-            wait(V, "gt%d" % t)
-        v(V.transpose(T.tb[:, y:y + 32 * n], T.lb[:, z:z + 32 * n]))
-        vw()
-        v(V.tensor_tensor(T.lv[:, q:q + n], T.tb[:, y:y + 32 * n:32], T.tb[:, y + 16:y + 32 * n:32], AL.min))
-        vw()
-        v(V.tensor_tensor(T.lw[:, 1:PW:2], T.lv[:, q:q + KC], T.lw[:, 0:PW:2], AL.min))
-        if t + 1 < R:
-            p = PW + 16 * t
-            v(V.tensor_tensor(T.lw[:, p + 1:p + 2 * LC:2], T.lv[:, q + KC:q + NL], T.lw[:, p:p + 2 * LC:2], AL.min))
-
-    lists_begin(0)
-    v(V.tensor_scalar(T.pe1[:, :], T.pe0[:, :], 1024.0 * (LC - 1) + 256.0 + NB + 1, None, AL.min))
-    wait(V, "tbc")
+    wait(V, "fla")
+    wait(V, "ioj")
     vw()
-    v(V.tensor_scalar(T.base[:, 0:R], T.thb[:, 0:R], -2.0, T.pe0[:, 0:1], AL.mult, AL.add))
-    v(V.tensor_scalar(T.base[:, R:2 * R], T.thb[:, 0:R], -2.0, T.pe1[:, 0:1], AL.mult, AL.add))
+    v(V.tensor_copy(T.la[:, 0:TW].indirect(T.bun[:, 0, 0:LC]), T.jval[:, :]), "sca")
+    v(V.tensor_scalar(T.lq[:, PW:PE:2], T.bun[:, 0, BK:BW], float(NB - LESS), None, AL.add))
+    wait(S, "sca")
+    up(S.activation(T.la[:, TW:LU], T.la[:, 0:TW].indirect(T.bun[:, 0, BG:BK]), AF.Copy), "gta")
+    wait(S, "gta")
+    for c, forms in enumerate((T.la[:, LW:LU], T.la[:, TW + 64 * ba + 16:TW + 64 * ba + 16 + B])):
+        for h in range(2):
+            up(S.activation(T.lz[:, :, 16 * h + c:16 * h + 16:2], forms, AF.Copy), "lzr")
+    wait(V, "sca")
+    v(V.transpose(T.ta[:, 0:TW], T.la[:, 0:TW]))
     wait(V, "urr")
     v(V.quantize_mx(T.uqc[:, :], T.uqs[:, :], T.ur[:, :]), "uq")
-    lists_end(0)
+    wait(V, "gta")
+    v(V.transpose(T.ta[:, TW:LW], T.la[:, TW:LW]))
+    vw()
+    v(V.tensor_tensor(T.lq[:, 1:PW:2], T.ta[:, 0:TW:32], T.ta[:, 16:TW:32], AL.min), "lqr")
+    v(V.tensor_copy(T.lq[:, PW + 1:PE:2], T.ta[:, TW:LW:32]), "lqr")
+
+    def spread(t, on_vector):
+        n = PA if t else PE
+        for k in range(4):
+            out, in_ = T.lw[q[k], t, 0:n], T.lq[q[t], 0:n]
+            up(V.tensor_copy(out, in_) if k < on_vector else S.activation(out, in_, AF.Copy), "lw%d" % t)
+
+    both("lqr")
+    spread(0, 2)
+    wait(V, "tbc")
+    v(V.tensor_scalar(T.base[:, 0:R], T.thb[:, 0:R], -2.0, T.pe0[:, 0:1], AL.mult, AL.add))
+    v(V.tensor_scalar(T.base[:, 2 * R:3 * R], T.thb[:, 0:R], -2.0, T.pe1[:, 0:1], AL.mult, AL.add))
+    vw()
+    v(V.tensor_scalar(T.base[:, R:2 * R], T.base[:, 0:R], 16 * 1024.0, None, AL.add))
+
+    def two_lists():
+        wait(V, "lzr")
+        v(V.transpose(T.tz[:, :, :], T.lz[:, :, :]))
+        vw()
+        v(V.tensor_copy(T.lq[:, PE:PA], T.tz[:, :, 0]), "lqa")
+        wait(S, "lqa")
+
+    def two_offsets(t):
+        wait(V, "lw%d" % t)
+        v(V.tensor_scalar(T.offa[:, 4 * t:4 * t + 4], T.lw[:, t, PE:PA], float(LESS), None, AL.add), "oa%d" % t)
 
     def quantize_w(t):
         wait(V, "wl%d" % t)
         for i in (2 * t, 2 * t + 1):
             v(V.quantize_mx(T.wqc[:, 128 * i:128 * i + 128], T.wqs[:, 128 * i:128 * i + 128], T.wt[:, 512 * i:512 * i + 512]), "wq%d" % t)
 
-    def product(i, bank, cols, win, name):
+    def last_offsets():
+        for k in range(1, 4):
+            v(V.tensor_copy(T.bun[q[k], R - 1, 0:LC], T.bun[q0, R - 1, 0:LC]))
+
+    def last_list():
+        wait(V, "flb")
+        v(V.tensor_copy(T.lb[:, :].indirect(T.bun[:, R - 1, 0:LC]), T.jval[:, :]))
+        vw()
+        v(V.transpose(T.tb[:, :], T.lb[:, :]))
+        vw()
+        wait(V, "lw%d" % (R - 2))
+        v(V.tensor_tensor(T.lq[:, 1:PW:2], T.tb[:, 0:TW:32], T.tb[:, 16:TW:32], AL.min))
+
+    BEHIND = ((lambda: quantize_w(1), lambda: two_offsets(1)),
+              (lambda: quantize_w(2), last_offsets, lambda: two_offsets(2), lambda: quantize_w(3)),
+              (last_list, lambda: two_offsets(3)),
+              (lambda: quantize_w(4),))
+    SHARED = (0, R - 2)
+    quantize_w(0)
+
+    def product(i, bank, a, b, win, name):
         p = 512 * bank
-        a, b = NB + cols[0], NB + cols[1]
         up(X.matmul_mx(T.psy[:, p:p + b - a], T.wqc[:, 128 * i:128 * i + 128], T.wqs[:, 128 * i:128 * i + 128], win[0][:, a:b], win[1][:, a:b], True, True), name)
 
     between(0)
+    OLD, END, NEW = 2, 3, 4
 
     for t in range(R):
         last = t + 1 == R
+        two = 0 < t < R - 1
         wc, ws = T["winc%d" % t], T["wins%d" % t]
-        nc, ns = T["winc%d" % (t + 1)], T["wins%d" % (t + 1)]
         if t == 0:
             wait(X, "uq")
             wait(X, "xq")
         wait(X, "arr%d" % t)
         bank = 512 * (t % 2)
         up(X.matmul_mx(T.psc[:, bank:bank + 128], T.uqc[:, :], T.uqs[:, :], wc[:, 0:128], ws[:, 0:128], True, True), "sco%d" % t)
+        if two:
+            tc, ts = T["twoc%d" % t], T["twos%d" % t]
+            for name in ("oa%d" % t, "tc%d" % (t - 1), "ts%d" % (t - 1), "arr%d" % t):
+                both(name)
+            pick(tc[:, :], ts[:, :], wc[:, :], ws[:, :], T.offa[:, 4 * t:4 * t + 4], ("two%d" % t,) * 2)
         wait(S, "sco%d" % t)
         up(S.activation(T.sg[:, NB * t:NB * t + NB], T.psc[:, bank:bank + NB], AF.Sign, bias=-1e-30, scale=-1.0, accum_out=T.cnt[:, t:t + 1]), "act%d" % t)
+        if last:
+            product(O * t, NEW, 0, 128, (wc, ws), "nm")
+            wait(S, "nm")
+            up(S.activation(T.yw[:, 0:128], T.psy[:, 512 * NEW:512 * NEW + 128], AF.Copy), "ne")
         vw()
-        wait(V, "act%d" % t)
-        v(V.tensor_scalar(T.idx[:, 4 * t:4 * t + 4:2], T.base[:, t:2 * R:R], T.cnt[:, t:t + 1], 1.0 / 512, AL.subtract, AL.mult))
-        vw()
+        if two:
+            both("two%d" % t)
         if not last:
-            v(V.tensor_copy(T.offs[:, 16 * t:16 * t + 16], T.lw[:, PW + 16 * t:PW + 16 * t + 2 * LC].indirect(T.idx[:, 4 * t + 2:4 * t + 3])), "ofr%d" % t)
-            wait(V, "ofr%d" % t)
-            oc = T.offs[:, 16 * t:16 * t + LC]
-            v(V.tensor_copy(T["sndc%d" % (t + 1)][:, :].bitcast(dt.uint32), wc[:, :].bitcast(dt.uint32).indirect(oc)), "pc%d" % (t + 1))
-            wait(S, "ofr%d" % t)
-            up(S.activation(T["snds%d" % (t + 1)][:, :], ws[:, :].indirect(oc), AF.Copy), "ps%d" % (t + 1))
+            wait(V, "lw%d" % t)
+        wait(V, "act%d" % t)
+        v(V.tensor_scalar(T.idx[:, 4 * t:4 * t + 3], T.base[:, t:3 * R:R], T.cnt[:, t:t + 1], 1.0 / 512, AL.subtract, AL.mult), "ix%d" % t)
+        wait(V, "ix%d" % t)
+        if two:
+            wait(S, "ix%d" % t)
+            pick_hop(t + 1, True, tc[:, :], ts[:, :], lambda a, b: T.idx[:, 4 * t:4 * t + 2])
+        if not last:
+            v(V.tensor_scalar(T["offs%d" % t][:, :], T.lw[:, t, PW:PE].indirect(T.idx[:, 4 * t + 2:4 * t + 3]), float(LESS), None, AL.add), "ofr%d" % t)
+            both("ofr%d" % t)
+            for first in (False,) if two else (True, False):
+                pick_hop(t + 1, first, wc[:, :], ws[:, :], lambda a, b: T["offs%d" % t][:, a:b])
             send(t + 1)
-            if t + 2 < R:
-                fill(t + 2)
-        v(V.tensor_copy(T.offt[:, 16 * t:16 * t + 16], T.lw[:, 0:PW].indirect(T.idx[:, 4 * t:4 * t + 1])), "ew%d" % t)
-        wait(V, "ew%d" % t)
-        wait(S, "ew%d" % t)
+        pairs = T.lq[:, 0:PW] if last else T.lw[:, t, 0:PW]
+        v(V.tensor_scalar(T.offt[:, 16 * t:16 * t + 16], pairs.indirect(T.idx[:, 4 * t:4 * t + 1]), float(LESS), None, AL.add), "ew%d" % t)
+        both("ew%d" % t)
         if last:
             break
-        oc = T.offt[:, 16 * t:16 * t + KC]
-        v(V.tensor_copy(nc[:, NB:WIN].bitcast(dt.uint32), wc[:, :].bitcast(dt.uint32).indirect(oc)), "tc%d" % t)
-        up(S.activation(ns[:, NB:WIN], ws[:, :].indirect(oc), AF.Copy), "ts%d" % t)
-        lists_begin(t + 1)
-        quantize_w(t)
-        if t == R - 2:
-            quantize_w(t + 1)
-        lists_end(t + 1)
+        nc, ns = T["winc%d" % (t + 1)], T["wins%d" % (t + 1)]
+        pick(nc[:, NB:WIN], ns[:, NB:WIN], wc[:, :], ws[:, :], T.offt[:, 16 * t:16 * t + KC], ("tc%d" % t, "ts%d" % t))
+        if t == 0:
+            two_lists()
+        if t + 2 < R:
+            spread(t + 1, 0)
+        for work in BEHIND[t]:
+            work()
         wait(X, "tc%d" % t)
         wait(X, "ts%d" % t)
         wait(X, "wq%d" % t)
         if t >= 3:
             wait(X, "ev%d" % (t - 3))
-        for o in range(O):
+        for o, name in enumerate(("ym%d" % t, "yn%d" % t)):
             i = O * t + o
-            product(i, i % 6, (0, K), (nc, ns), "ym%d" % t)
-        wait(S, "ym%d" % t)
-        for o in range(O):
-            i = O * t + o
-            up(S.activation(T.ysb[:, K * i:K * i + K], T.psy[:, 512 * (i % 6):512 * (i % 6) + K], AF.Copy), "ev%d" % t)
+            product(i, i % 6, NB, WIN, (nc, ns), name)
+            out, in_ = T.ysb[:, K * i:K * i + K], T.psy[:, 512 * (i % 6):512 * (i % 6) + K]
+            on = V if o and t in SHARED else S
+            wait(on, name)
+            up(V.tensor_copy(out, in_) if on is V else S.activation(out, in_, AF.Copy), "ev%d" % t)
+        if t == R - 2:
+            wait(X, "wq%d" % (t + 1))
+            wait(X, "ev1")
+            wait(X, "ev2")
+            product(O * (t + 1), OLD, 128, WIN, (nc, ns), "om")
+            wait(S, "om")
+            up(S.activation(T.yw[:, 128:WIN], T.psy[:, 512 * OLD:512 * OLD + WIN - 128], AF.Copy), "oe")
         between(t + 1)
 
     t = R - 1
+    half = [T.offt[:, 16 * t + KC // 2 * h:16 * t + KC // 2 * (h + 1)] for h in range(2)]
+    part = [slice(K * O * t + HK * i, K * O * t + HK * (i + 1)) for i in range(4)]
+    both("oe")
+    both("ne")
+    v(V.tensor_copy(T.ysb[:, part[0]], T.yw[:, :].indirect(half[0])), "lp")
+    up(S.activation(T.ysb[:, part[1]], T.yw[:, :].indirect(half[1]), AF.Copy), "lp")
     for h in range(2):
-        oc = T.offt[:, 16 * t + KC // 2 * h:16 * t + KC // 2 * (h + 1)]
-        at = slice(NB + HK * h, NB + HK * h + HK)
-        v(V.tensor_copy(nc[:, at].bitcast(dt.uint32), wc[:, :].bitcast(dt.uint32).indirect(oc)), "lc%d" % h)
-        up(S.activation(ns[:, at], ws[:, :].indirect(oc), AF.Copy), "ls%d" % h)
-    wait(X, "wq%d" % t)
-    wait(X, "ev1")
-    wait(X, "ev2")
-    for h in range(2):
+        at = slice(HK * h, HK * h + HK)
+        pick(T.endc[:, at], T.ends[:, at], wc[:, :], ws[:, :], half[h], ("lc%d" % h,) * 2)
         wait(X, "lc%d" % h)
-        wait(X, "ls%d" % h)
-        for o in range(O):
-            product(O * t + o, 2 + 2 * h + o, (HK * h, HK * h + HK), (nc, ns), "lm%d%d" % (h, o))
-    for h in range(2):
-        for o in range(O):
-            p = 512 * (2 + 2 * h + o)
-            c = K * (O * t + o) + HK * h
-            wait(V if o else S, "lm%d%d" % (h, o))
-            if o:
-                v(V.tensor_copy(T.ysb[:, c:c + HK], T.psy[:, p:p + HK]), "le%d%d" % (h, o))
-            else:
-                up(S.activation(T.ysb[:, c:c + HK], T.psy[:, p:p + HK], AF.Copy), "le%d%d" % (h, o))
-    for h in range(2):
-        for o in range(O):
-            c = K * (O * t + o) + HK * h
-            on = S if h == 1 and o == 0 else Y
-            wait(on, "le%d%d" % (h, o))
-            up(on.dma_start(T.y[:, c:c + HK], T.ysb[:, c:c + HK]), "kq" if on is S else "yl", 16)
+        product(O * t + 1, END + 2 * h, HK * h, HK * h + HK, (T.endc, T.ends), "lm%d" % h)
+    wait(V, "lm0")
+    v(V.tensor_copy(T.ysb[:, part[2]], T.psy[:, 512 * END:512 * END + HK]), "le0")
+    wait(S, "lm1")
+    up(S.activation(T.ysb[:, part[3]], T.psy[:, 512 * (END + 2):512 * (END + 2) + HK], AF.Copy), "le1")
+    for on, ready, at, done in ((Y, "lp", slice(part[0].start, part[1].stop), "yl"), (Y, "le0", part[2], "yl"), (S, "le1", part[3], "kq")):
+        wait(on, ready)
+        up(on.dma_start(T.y[:, at], T.ysb[:, at]), done, 16)
     for name in total:
         if waited.get(name, 0) < total[name]:
             wait(Y, name)

@@ -4,37 +4,37 @@ from concourse.mybir import dt, AluOpType, ActivationFunctionType
 N, K, B, R, O = 4, 256, 32, 5, 2
 NB = (N - 1) * B
 LC = NB // 16
+RC = 2 * N
 KC = K // 16
-TW = 2 * K
-GW = 2 * NB
-LW = TW + GW
-LU = LW + B
+TS, GS = KC + 2, RC + 2
+TW, GW = 16 * TS, 16 * GS
 HK = K // 2
 WIN = NB + K
-BG, BK = LC, 3 * LC + 2
-BW = BK + LC
-PW = 2 * KC
-PE = PW + 2 * LC
-PA = PE + 4
-LESS = 128
+PS, PT = 8, 32
+PE = PT + 2 * TS
+IX = 6
+EARLY = (2, 3)
+TURN = 256.0 + NB + 1
 
 SCRATCH = {
     "psc": ("psum", [128, 1024], "float32"),
     "psy": ("psum", [128, 3072], "float32"),
-    "ci": ("sbuf", [128, 2 * R, 8], "int32"), "cc": ("sbuf", [128, 2 * R, LC], "int32"), "ch": ("sbuf", [128, 2 * R, LC], "int32"),
-    "cp": ("sbuf", [128, 2 * R, LC], "float32"), "bun": ("sbuf", [128, R, BW], "uint16"), "lw": ("sbuf", [128, R - 1, PA], "float32"),
-    "lz": ("sbuf", [128, 4, 32], "bfloat16"), "tz": ("sbuf", [128, 4, 32], "bfloat16"),
+    "lw": ("sbuf", [128, R - 1, PE + 4], "float32"),
+    "lz": ("sbuf", [128, PS, 32], "bfloat16"), "tz": ("sbuf", [128, PS, 32], "bfloat16"),
 }
 for _n, _w, _d in (
         ("xt", 4 * K, "bfloat16"), ("ut", 16, "bfloat16"), ("ur", 512, "bfloat16"), ("zt", 128, "bfloat16"),
         ("uqc", 128, "float8_e4m3fn_x4"), ("uqs", 128, "uint8"),
         ("wt", 512 * R * O, "bfloat16"), ("wqc", 128 * R * O, "float8_e4m3fn_x4"), ("wqs", 128 * R * O, "uint8"),
-        ("of0", 8, "uint16"), ("thr1", 16, "int32"), ("thb", 16, "int32"),
-        ("pidx", KC, "int32"), ("p15", KC, "int32"), ("k16", KC, "int32"), ("oddi", 1, "int32"),
-        ("odd16", 1, "float32"), ("even16", 1, "float32"),
-        ("pe0", 1, "float32"), ("pe1", 1, "float32"), ("base", 3 * R, "float32"), ("jval", NB, "bfloat16"),
-        ("la", LU, "bfloat16"), ("ta", LW, "bfloat16"), ("lb", TW, "bfloat16"), ("tb", TW, "bfloat16"), ("lq", PA, "float32"),
-        ("idx", 4 * R, "uint16"), ("offt", 16 * R, "uint16"), ("offa", 4 * R, "uint16"),
+        ("ci", RC, "int32"), ("cqd", RC, "int32"), ("cqs", GS, "int32"), ("cqe", RC, "int32"),
+        ("of0", RC, "uint16"), ("bq", LC + GS, "uint16"), ("be", LC, "uint16"), ("thr1", 16, "int32"), ("thb", 16, "int32"),
+        ("pidx", TS, "int32"), ("p15", 1, "int32"), ("p31", TS, "int32"), ("kslot", TS, "int32"), ("oddi", 1, "int32"),
+        ("odd16", 1, "float32"), ("even16", 1, "float32"), ("slots", 32, "float32"), ("slot", 32, "float32"),
+        ("pe0", 1, "float32"), ("pe1", 1, "float32"), ("pe2", 1, "float32"), ("base", (IX - 1) * R, "float32"),
+        ("count", TW + NB - 16, "bfloat16"), ("la", TW, "bfloat16"), ("ta", TW, "bfloat16"), ("lb", TW, "bfloat16"), ("tb", TW, "bfloat16"),
+        ("lg", 2 * GW, "bfloat16"), ("tg", 2 * GW, "bfloat16"), ("lq", PE, "float32"),
+        ("idx", IX * R, "uint16"), ("offt", 16 * R, "uint16"), ("offa", PS * R, "uint16"),
+        ("offe", 32 * R, "uint16"), ("offg", 2 * R, "uint16"), ("forms", 4, "uint16"), ("less", 2, "float32"),
         ("sg", R * NB, "float32"), ("cnt", R, "float32"), ("ysb", R * O * K, "float32"),
         ("yw", WIN, "float32"), ("endc", K, "float8_e4m3fn_x4"), ("ends", K, "uint8")):
     SCRATCH[_n] = ("sbuf", [128, _w], _d)
@@ -42,17 +42,22 @@ for _t in range(R):
     SCRATCH["sndc%d" % _t] = ("sbuf", [128, N * B], "float8_e4m3fn_x4")
     SCRATCH["snds%d" % _t] = ("sbuf", [128, N * B], "uint8")
     SCRATCH["offs%d" % _t] = ("sbuf", [128, 16], "uint16")
-    SCRATCH["twoc%d" % _t] = ("sbuf", [128, 2 * B], "float8_e4m3fn_x4")
-    SCRATCH["twos%d" % _t] = ("sbuf", [128, 2 * B], "uint8")
+    SCRATCH["twoc%d" % _t] = ("sbuf", [128, 4 * B], "float8_e4m3fn_x4")
+    SCRATCH["twos%d" % _t] = ("sbuf", [128, 4 * B], "uint8")
     SCRATCH["winc%d" % _t] = ("sbuf", [128, WIN], "float8_e4m3fn_x4")
     SCRATCH["wins%d" % _t] = ("sbuf", [128, WIN], "uint8")
 
-SEMAPHORES = ["xl", "csl", "cdl", "ul", "thl", "iot", "iok", "ioj", "fla", "flb", "tbc", "ztr", "urr", "uq", "xq", "o0", "vq", "kq", "yl",
-              "sca", "gta", "lqr", "lqa", "lzr", "om", "oe", "nm", "ne", "lp"]
+SEMAPHORES = ["xl", "csl", "cdl", "cql", "cel", "ul", "iot", "iok", "ioc", "ios", "con", "pad", "fla", "flb", "tbc", "ztr", "urr", "uq",
+              "xq", "o0", "vq", "kq", "yl", "bqr", "sca", "gu", "gc", "lqr", "lzr", "om", "oe", "nm", "ne"]
 for _t in range(R):
-    SEMAPHORES += ["%s%d" % (n, _t) for n in ("arr", "snt", "pa", "pb", "ps", "two", "ix", "oa", "tc", "ts", "sco", "act", "ofr",
-                                              "wl", "wq", "ym", "yn", "ev", "ew", "lw")]
-SEMAPHORES += ["%s%d" % (n, o) for n in ("lm", "le", "lc") for o in range(2)]
+    SEMAPHORES += ["%s%d" % (n, _t) for n in ("arr", "snt", "pc0", "pc1", "pc2", "ps0", "ps1", "ps2", "ix", "sco", "act", "wl", "wq", "ew")]
+    SEMAPHORES += ["%s%d" % (n, _t) for n in ("two", "oa", "tc", "ts", "ofr", "ym", "yn", "ev", "lw") if _t < R - 1]
+SEMAPHORES += ["%s%d" % (n, o) for n in ("lm", "le", "lc") for o in range(2)] + ["lp0"]
+for _t in EARLY:
+    SCRATCH["gotc%d" % _t] = ("sbuf", [128, 2 * B], "float8_e4m3fn_x4")
+    SCRATCH["gots%d" % _t] = ("sbuf", [128, 2 * B], "uint8")
+    SCRATCH["goti%d" % _t] = ("sbuf", [128, 2], "uint16")
+    SEMAPHORES += ["arp%d" % _t, "got%d" % _t]
 
 AL = AluOpType
 AF = ActivationFunctionType
@@ -92,42 +97,42 @@ def rank_program(g, core, T, topo):
         wait(Y, "ev%d" % t)
         up(Y.dma_start(T.y[:, O * K * t:O * K * (t + 1)], T.ysb[:, O * K * t:O * K * (t + 1)]), "yl", 16)
 
-    BETWEEN = ((("w", 1), ("w", 2)), (("w", 3), ("y", 0)), (("w", 4), ("y", 1)), (("y", 2),), (("y", 3),))
+    def load_list(on, out, a, keys, t, name):
+        up(on.dma_start(out, keys[:, RC * t:RC * (t + 1)]), name, 16)
 
-    def between(t):
-        wait(Y, "snt%d" % t)
-        for kind, i in BETWEEN[t]:
-            (load_w if kind == "w" else store_y)(i)
+    def load_last(_):
+        for a in range(8):
+            load_list(Y, T.cqe[16 * a:16 * a + 16, :], a, T.cd, R - 1, "cel")
 
-    up(Y.dma_start(T.ci[0:16, 0:R, :], T.cs[:, :]), "csl", 16)
-    up(S.dma_start(T.ci[16:32, 0:R, :], T.cs[:, :]), "csl", 16)
+    v(V.memset(T.cqs[:, :], 0), "pad")
+    for a in range(2):
+        load_list(S if a else Y, T.ci[16 * a:16 * a + 16, :], a, T.cs, 0, "csl")
     up(Y.dma_start(T.xt[:, :], T.x[:, :]), "xl", 16)
-    up(S.dma_start(T.ci[0:16, R:2 * R, :], T.cd[:, :]), "cdl", 16)
-    up(S.dma_start(T.ci[16:32, R:2 * R, :], T.cd[:, :]), "cdl", 16)
     up(Y.dma_start(T.ut[:, :], T.u[:, 0:16]), "ul", 16)
-    up(Y.dma_start(T.thr1[0:1, :], T.thr[:, :]), "thl", 16)
+    up(Y.dma_start(T.thr1[0:1, :], T.thr[:, :]), "ul", 16)
+    wait(Y, "pad")
+    for a in range(8):
+        load_list(S, T.cqd[16 * a:16 * a + 16, :], a, T.cd, a // 2, "cdl")
+        load_list(Y, T.cqs[16 * a:16 * a + 16, a % 2:a % 2 + RC], a, T.cs, a // 2 + 1, "cql")
     load_w(0)
+    load_w(1)
 
-    def fill(table, n, name):
-        up(g.iota(table[:, 0:32 * n], [[16, n], [0, 2], [1, 16]], NB - LESS, 0, allow_small_or_imprecise_dtypes=True), name)
-
-    up(g.iota(T.pidx[:, :], [[0, KC]], 0, 1), "iot")
-    up(g.iota(T.k16[:, :], [[16, KC]], NB - LESS, 0), "iok")
-    fill(T.la, KC // 4, "fla")
-    up(g.iota(T.jval[:, :], [[1, NB]], -LESS, 0, allow_small_or_imprecise_dtypes=True), "ioj")
+    up(g.iota(T.pidx[:, :], [[0, TS]], 0, 1), "iot")
+    up(g.iota(T.kslot[:, :], [[32, TS // 2], [-16, 2]], 0, 0), "iok")
+    up(g.iota(T.count[:, :], [[1, TW + NB - 16]], -NB, 0, allow_small_or_imprecise_dtypes=True), "ioc")
 
     v(V.memset(T.zt[:, :], 0.0), "ztr")
+    v(V.memset(T.lq[:, PS + 2 * GS:PT], 0.0))
     wait(V, "iot")
-    v(V.tensor_scalar(T.p15[:, :], T.pidx[:, :], 15, None, AL.bitwise_and))
     v(V.tensor_scalar(T.oddi[:, :], T.pidx[:, 0:1], 16, None, AL.bitwise_and))
+    v(V.tensor_scalar(T.p31[:, :], T.pidx[:, :], 31, None, AL.bitwise_and))
     vw()
-    v(V.tensor_scalar(T.pe0[:, :], T.p15[:, 0:1], 1024.0, 256.0 + NB + 1, AL.mult, AL.add))
+    v(V.tensor_scalar(T.even16[:, :], T.oddi[:, :], -1.0, 16.0, AL.mult, AL.add), "con")
     v(V.tensor_copy(T.odd16[:, :], T.oddi[:, :]))
-    v(V.tensor_scalar(T.even16[:, :], T.oddi[:, :], -1.0, 16.0, AL.mult, AL.add))
-    wait(V, "iok")
-    v(V.tensor_tensor(T.lq[:, 0:PW:2], T.p15[:, :], T.k16[:, :], AL.add))
-    vw()
-    v(V.tensor_scalar(T.pe1[:, :], T.pe0[:, :], 1024.0 * (LC - 1) + 256.0 + NB + 1, None, AL.min))
+    wait(S, "ioc")
+    wait(S, "con")
+    for table, name in ((T.lb, "flb"), (T.la, "fla")):
+        up(S.activation(table[:, :], T.count[:, NB - 16:], AF.Identity, bias=T.even16[:, 0:1]), name)
 
     def roles(s):
         rest = [d for d in range(N) if d != s]
@@ -139,137 +144,163 @@ def rank_program(g, core, T, topo):
     if r < N - 1:
         runs.append((2 * r + 2, 2 * r, LC - 2 * r))
     q = [slice(32 * k, 32 * k + 32) for k in range(4)]
+    giver = [s for s in others if roles(s)[0] == r][0]
 
     wait(V, "csl")
     for k in range(4):
-        v(V.tensor_copy(T.of0[q[k], :], T.ci[q[0], 0, :]), "o0")
+        v(V.tensor_copy(T.of0[q[k], :], T.ci[q[0], :]), "o0")
     wait(V, "xl")
     v(V.quantize_mx(T.winc0[:, NB:WIN], T.wins0[:, NB:WIN], T.xt[:, :]), "xq")
-
-    def block(t, role):
-        d = roles(r)[role]
-        return d if t == 0 else others.index(d)
 
     def pick(codes, scales, wc, ws, oc, names):
         v(V.tensor_copy(codes.bitcast(dt.uint32), wc.bitcast(dt.uint32).indirect(oc)), names[0])
         up(S.activation(scales, ws.indirect(oc), AF.Copy), names[1])
 
-    def pick_hop(t, first, wc, ws, oc):
-        b, n = (block(t, 0), 1) if first else (min(block(t, 1), block(t, 2)), 2)
-        at = slice(B * b, B * (b + n))
-        pick(T["sndc%d" % t][:, at], T["snds%d" % t][:, at], wc, ws, oc(2 * b, 2 * (b + n)), ("p%s%d" % ("a" if first else "b", t), "ps%d" % t))
+    def pick_hop(t, role, wc, ws, oc):
+        at = slice(B * roles(r)[role], B * roles(r)[role] + B)
+        pick(T["sndc%d" % t][:, at], T["snds%d" % t][:, at], wc, ws, oc, ["p%s%d%d" % (n, role, t) for n in "cs"])
 
     both("o0")
     both("xq")
-    for first in (True, False):
-        pick_hop(0, first, T.winc0[:, NB:WIN], T.wins0[:, NB:WIN], lambda a, b: T.of0[:, a:b])
+    for role, d in enumerate(roles(r)):
+        pick_hop(0, role, T.winc0[:, NB:WIN], T.wins0[:, NB:WIN], T.of0[:, 2 * d:2 * d + 2])
 
-    PLAN = (("a", "c", ((0, 0, 1),)), ("b", "c", ((1, 0, 2), (2, 1, 2))), ("s", "s", ((0, 0, 2), (1, 1, 2))), ("s", "s", ((2, 0, 1),)))
+    PLAN = [[("c", 0, 0, 1)], [("c", 1, 0, 1)], [("s", 0, 0, 2), ("s", 1, 1, 2)], [("c", 2, 0, 1)], [("s", 2, 0, 1)]]
+    FIRST = [[("c", 0, 0, 2)], [("c", 1, 1, 2)]] + PLAN[2:]
+    LATE = [[(kind, role, 0, 1)] for role in (1, 2) for kind in "cs"]
 
     def engines(s, role, first, step):
         return topo.engines(T.cores[s], T.cores[roles(s)[role]])[first::step]
 
-    def piece(kind, t, role, first, step):
+    def piece(t, kind, role, first, step):
+        wait(g, "p%s%d%d" % (kind, role, t))
         d = roles(r)[role]
         rid, pid, _ = topo.addr(T.cores[d])
-        b = block(t, role)
         at = B * (r if r < d else r - 1)
-        src = T["snd%s%d" % (kind, t)][:, B * b:B * b + B]
+        src = T["snd%s%d" % (kind, t)][:, B * d:B * d + B]
         dst = T["win%s%d" % (kind, t)][:, at:at + B]
         if kind == "c":
             src, dst = src.bitcast(dt.uint8), dst.bitcast(dt.uint8)
         return RemoteDMATransfer(dst_ids=[DstId(rid=rid, pnc=pid)], dma_engine_mask=sum(1 << e for e in engines(r, role, first, step)),
                                  remote_sem=T.sem["arr%d" % t], srcs=[src], dsts=[dst])
 
+    def send_early(t, ready, src, dst):
+        wait(g, ready)
+        rid, pid, _ = topo.addr(T.cores[roles(r)[0]])
+        g.remote_dma(dst, src, T.sem["arp%d" % t], T.sem["snt%d" % t], pid, rid, topo.mask(core, T.cores[roles(r)[0]]))
+        total["snt%d" % t] = total.get("snt%d" % t, 0) + len(engines(r, 0, 0, 1))
+        total["arp%d" % t] = total.get("arp%d" % t, 0) + len(engines(giver, 0, 0, 1))
+
     def send(t):
-        n = 0
-        for i, (ready, kind, tr) in enumerate(PLAN):
-            if i == 0 or PLAN[i - 1][0] != ready:
-                wait(g, "p%s%d" % (ready, t))
-            g.remote_dma_fused([piece(kind, t, *p) for p in tr], local_sem=T.sem["snt%d" % t])
-            n += sum(len(engines(r, *p)) for p in tr)
-        total["snt%d" % t] = n
-        total["arr%d" % t] = sum(len(engines(s, *p)) for s in others for _, _, tr in PLAN for p in tr if roles(s)[p[0]] == r)
+        plan = []
+        for call in LATE if t in EARLY else PLAN if t else FIRST:
+            g.remote_dma_fused([piece(t, *p) for p in call], local_sem=T.sem["snt%d" % t])
+            plan += call
+        total["snt%d" % t] = total.get("snt%d" % t, 0) + sum(len(engines(r, *p[1:])) for p in plan)
+        total["arr%d" % t] = sum(len(engines(s, *p[1:])) for s in others for p in plan if roles(s)[p[1]] == r)
 
     send(0)
 
-    wait(g, "thl")
+    for o, (step, first) in enumerate(((3, 0), (-1, 1))):
+        up(g.iota(T.slots[:, 16 * o:16 * o + 16], [[2048, 8], [1024 * step, 2]], int(TURN) + 1024 * first, 0, allow_small_or_imprecise_dtypes=True), "ios")
+    wait(g, "ul")
     up(g.partition_broadcast(T.thb[:, :], T.thr1[0:1, :], 128), "tbc")
-    fill(T.lb, KC, "flb")
 
-    for n in (TW // 4, TW // 2):
-        wait(S, "fla")
-        up(S.activation(T.la[:, n:2 * n], T.la[:, 0:n], AF.Identity, bias=float(n // 2)), "fla")
-
-    wait(S, "ul")
-    wait(S, "ztr")
-    for i in range(4):
+    def repeat_u(i):
         up(S.activation(T.ur[:, i:512:4], T.zt[:, :], AF.Identity, bias=T.ut[:, i:i + 1]), "urr")
 
-    q0, there, here = q[0], slice(1, R), slice(R, 2 * R)
-    ba = block(1, 0)
+    def interleave(c):
+        for i, d in enumerate(roles(r)[:2]):
+            for h in range(2):
+                up(S.activation(T.lz[:, 4 * i:4 * i + 4, 16 * h + c:16 * h + 16:2], T.lg[:, GW * c + B * d:GW * c + B * d + B], AF.Copy), "lzr")
+
+    vw()
+    wait(V, "cql")
+    v(V.tensor_scalar(T.bq[:, LC:], T.cqs[:, :], T.odd16[:, 0:1], None, AL.add), "bqr")
     wait(V, "cdl")
     for a, b, n in runs:
-        v(V.tensor_copy(T.cc[q0, 1:, b:b + n], T.ci[q0, 1:, a:a + n]))
-    vw()
-    v(V.tensor_scalar(T.ch[q0, 1:, :], T.cc[q0, 1:, :], 240, None, AL.bitwise_and))
-    v(V.tensor_copy(T.bun[q0, 0:R - 1, BK:BW], T.cc[q0, there, :]))
-    vw()
-    v(V.tensor_tensor(T.cp[q0, 1:, :], T.cc[q0, 1:, :], T.ch[q0, 1:, :], AL.add))
-    vw()
-    v(V.tensor_scalar(T.bun[q0, :, 0:LC], T.cp[q0, here, :], T.odd16[q0, 0:1], None, AL.add))
-    for i in range(2):
-        v(V.tensor_scalar(T.bun[q0, 0:R - 1, BG + i:BK - 2:2], T.cp[q0, there, :], T.odd16[q0, 0:1], None, AL.add))
-    v(V.tensor_scalar(T.bun[q0, 0:R - 1, BK - 2:BK], T.cp[q0, there, 2 * ba:2 * ba + 2], T.even16[q0, 0:1], None, AL.add))
-    vw()
-    for k in range(1, 4):
-        v(V.tensor_copy(T.bun[q[k], 0, :], T.bun[q0, k, :]))
-
+        v(V.tensor_scalar(T.bq[:, b:b + n], T.cqd[:, a:a + n], T.odd16[:, 0:1], None, AL.add))
     wait(V, "fla")
-    wait(V, "ioj")
     vw()
-    v(V.tensor_copy(T.la[:, 0:TW].indirect(T.bun[:, 0, 0:LC]), T.jval[:, :]), "sca")
-    v(V.tensor_scalar(T.lq[:, PW:PE:2], T.bun[:, 0, BK:BW], float(NB - LESS), None, AL.add))
-    wait(S, "sca")
-    up(S.activation(T.la[:, TW:LU], T.la[:, 0:TW].indirect(T.bun[:, 0, BG:BK]), AF.Copy), "gta")
-    wait(S, "gta")
-    for c, forms in enumerate((T.la[:, LW:LU], T.la[:, TW + 64 * ba + 16:TW + 64 * ba + 16 + B])):
-        for h in range(2):
-            up(S.activation(T.lz[:, :, 16 * h + c:16 * h + 16:2], forms, AF.Copy), "lzr")
+    v(V.tensor_copy(T.la[:, :].indirect(T.bq[:, 0:LC]), T.count[:, 0:NB]), "sca")
+    wait(S, "ul")
+    wait(S, "ztr")
+    repeat_u(0)
+    for c, (table, ready, name) in enumerate(((T.lb, ("flb", "bqr"), "gu"), (T.la, ("sca",), "gc"))):
+        for n in ready:
+            wait(S, n)
+        up(S.activation(T.lg[:, GW * c:GW * c + GW], table[:, :].indirect(T.bq[:, LC:]), AF.Copy), name)
+        wait(S, name)
+        interleave(c)
+    for i in range(1, 4):
+        repeat_u(i)
     wait(V, "sca")
-    v(V.transpose(T.ta[:, 0:TW], T.la[:, 0:TW]))
-    wait(V, "urr")
-    v(V.quantize_mx(T.uqc[:, :], T.uqs[:, :], T.ur[:, :]), "uq")
-    wait(V, "gta")
-    v(V.transpose(T.ta[:, TW:LW], T.la[:, TW:LW]))
+    v(V.transpose(T.ta[:, :], T.la[:, :]))
+    wait(V, "iok")
+    v(V.tensor_tensor(T.lq[:, PT:PE:2], T.p31[:, :], T.kslot[:, :], AL.add), "lqr")
+    v(V.tensor_scalar(T.p15[:, :], T.pidx[:, 0:1], 15, None, AL.bitwise_and))
     vw()
-    v(V.tensor_tensor(T.lq[:, 1:PW:2], T.ta[:, 0:TW:32], T.ta[:, 16:TW:32], AL.min), "lqr")
-    v(V.tensor_copy(T.lq[:, PW + 1:PE:2], T.ta[:, TW:LW:32]), "lqr")
-
-    def spread(t, on_vector):
-        n = PA if t else PE
-        for k in range(4):
-            out, in_ = T.lw[q[k], t, 0:n], T.lq[q[t], 0:n]
-            up(V.tensor_copy(out, in_) if k < on_vector else S.activation(out, in_, AF.Copy), "lw%d" % t)
-
-    both("lqr")
-    spread(0, 2)
-    wait(V, "tbc")
-    v(V.tensor_scalar(T.base[:, 0:R], T.thb[:, 0:R], -2.0, T.pe0[:, 0:1], AL.mult, AL.add))
-    v(V.tensor_scalar(T.base[:, 2 * R:3 * R], T.thb[:, 0:R], -2.0, T.pe1[:, 0:1], AL.mult, AL.add))
+    v(V.tensor_copy(T.lq[:, PT + 1:PE:2], T.ta[:, 0:TW:16]), "lqr")
+    v(V.tensor_scalar(T.pe0[:, :], T.p15[:, :], 1024.0, TURN, AL.mult, AL.add))
+    v(V.tensor_scalar(T.pe1[:, :], T.p15[:, :], 1024.0, TURN + 16 * 1024, AL.mult, AL.add))
+    wait(V, "gu")
+    wait(V, "gc")
+    v(V.transpose(T.tg[:, :], T.lg[:, :]))
+    wait(V, "lzr")
+    v(V.transpose(T.tz[:, :, :], T.lz[:, :, :]))
     vw()
-    v(V.tensor_scalar(T.base[:, R:2 * R], T.base[:, 0:R], 16 * 1024.0, None, AL.add))
-
-    def two_lists():
-        wait(V, "lzr")
-        v(V.transpose(T.tz[:, :, :], T.lz[:, :, :]))
-        vw()
-        v(V.tensor_copy(T.lq[:, PE:PA], T.tz[:, :, 0]), "lqa")
-        wait(S, "lqa")
+    for c in range(2):
+        v(V.tensor_copy(T.lq[:, PS + c:PS + 2 * GS:2], T.tg[:, GW * c:GW * c + GW:16]), "lqr")
+    v(V.tensor_copy(T.lq[:, 0:PS], T.tz[:, :, 0]), "lqr")
+    for k in range(4):
+        v(V.tensor_scalar(T.offa[q[k], 0:PS], T.tz[q[0], :, 0], float(NB), None, AL.add), "oa0")
 
     def two_offsets(t):
         wait(V, "lw%d" % t)
-        v(V.tensor_scalar(T.offa[:, 4 * t:4 * t + 4], T.lw[:, t, PE:PA], float(LESS), None, AL.add), "oa%d" % t)
+        v(V.tensor_scalar(T.offa[:, PS * t:PS * t + PS], T.lw[:, t, 0:PS], float(NB), None, AL.add), "oa%d" % t)
+        if t + 1 in EARLY:
+            for c in range(2):
+                v(V.tensor_scalar(T.offe[:, 32 * t + 16 * c:32 * t + 16 * c + 16], T.lw[:, t, PS:PS + 2 * GS].indirect(T.forms[:, 2 * c:2 * c + 1]),
+                                  float(NB * c), None, AL.add), "oa%d" % t)
+            for name in ("oa%d" % t, "tc%d" % (t - 1), "ts%d" % (t - 1)):
+                both(name)
+            form_early(t, 0, T["winc%d" % t][:, NB:WIN], T["wins%d" % t][:, NB:WIN])
+
+    def form_early(t, c, wc, ws):
+        at, e = slice(B * c, B * c + B), 32 * t + 16 * c + 2 * roles(r)[0]
+        tc, ts = T["twoc%d" % t][:, at], T["twos%d" % t][:, at]
+        pick(tc, ts, wc, ws, T.offe[:, e:e + 2], ("pc0%d" % (t + 1), "ps0%d" % (t + 1)))
+        send_early(t + 1, "pc0%d" % (t + 1), tc.bitcast(dt.uint8), T["gotc%d" % (t + 1)][:, at].bitcast(dt.uint8))
+        send_early(t + 1, "ps0%d" % (t + 1), ts, T["gots%d" % (t + 1)][:, at])
+
+    def spread(t):
+        for k in range(4):
+            out, in_ = T.lw[q[k], t, 0:PE], T.lq[q[t], :]
+            if t < 2:
+                up(S.activation(out, in_, AF.Copy), "lw%d" % t)
+            else:
+                up(Y.dma_start(out, in_), "lw%d" % t, 16)
+
+    wait(V, "urr")
+    v(V.quantize_mx(T.uqc[:, :], T.uqs[:, :], T.ur[:, :]), "uq")
+    wait(S, "lqr")
+    spread(0)
+    wait(V, "ios")
+    v(V.transpose(T.slot[:, :], T.slots[:, :]))
+    wait(V, "tbc")
+    v(V.tensor_scalar(T.base[:, 0:R], T.thb[:, 0:R], -2.0, T.pe0[:, 0:1], AL.mult, AL.add))
+    v(V.tensor_scalar(T.base[:, R:2 * R], T.thb[:, 0:R], -2.0, T.pe1[:, 0:1], AL.mult, AL.add))
+    vw()
+    v(V.tensor_scalar(T.pe2[:, :], T.slot[:, 0:1], 1024.0 * (GS - 1) + TURN, None, AL.min))
+    v(V.tensor_scalar(T.base[:, 4 * R:5 * R], T.thb[:, 0:R], -2.0, T.slot[:, 0:1], AL.mult, AL.add))
+    vw()
+    v(V.tensor_scalar(T.base[:, 2 * R:4 * R], T.thb[:, 0:2 * R], -2.0, T.pe2[:, 0:1], AL.mult, AL.add))
+
+    def early_constants():
+        for c in range(2):
+            v(V.tensor_scalar(T.forms[:, 2 * c:2 * c + 1], T.pe2[:, :], 512.0 * c - TURN, 1.0 / 512, AL.add, AL.mult))
+            v(V.tensor_scalar(T.less[:, c:c + 1], T.p15[:, :], 63.0, 63.0 * 16 * c, AL.mult, AL.add))
+        vw()
 
     def quantize_w(t):
         wait(V, "wl%d" % t)
@@ -277,81 +308,120 @@ def rank_program(g, core, T, topo):
             v(V.quantize_mx(T.wqc[:, 128 * i:128 * i + 128], T.wqs[:, 128 * i:128 * i + 128], T.wt[:, 512 * i:512 * i + 512]), "wq%d" % t)
 
     def last_offsets():
-        for k in range(1, 4):
-            v(V.tensor_copy(T.bun[q[k], R - 1, 0:LC], T.bun[q0, R - 1, 0:LC]))
+        wait(V, "cel")
+        for a, b, n in runs:
+            v(V.tensor_scalar(T.be[:, b:b + n], T.cqe[:, a:a + n], T.odd16[:, 0:1], None, AL.add))
+
+    def last_scatter():
+        v(V.tensor_copy(T.lb[:, :].indirect(T.be[:, :]), T.count[:, 0:NB]))
 
     def last_list():
-        wait(V, "flb")
-        v(V.tensor_copy(T.lb[:, :].indirect(T.bun[:, R - 1, 0:LC]), T.jval[:, :]))
-        vw()
         v(V.transpose(T.tb[:, :], T.lb[:, :]))
+        two_offsets(R - 2)
+        quantize_w(R - 2)
         vw()
-        wait(V, "lw%d" % (R - 2))
-        v(V.tensor_tensor(T.lq[:, 1:PW:2], T.tb[:, 0:TW:32], T.tb[:, 16:TW:32], AL.min))
+        v(V.tensor_copy(T.lq[:, PT + 1:PE:2], T.tb[:, 0:TW:16]))
 
-    BEHIND = ((lambda: quantize_w(1), lambda: two_offsets(1)),
-              (lambda: quantize_w(2), last_offsets, lambda: two_offsets(2), lambda: quantize_w(3)),
-              (last_list, lambda: two_offsets(3)),
-              (lambda: quantize_w(4),))
-    SHARED = (0, R - 2)
     quantize_w(0)
+    BEHIND = ((early_constants, lambda: two_offsets(1), lambda: quantize_w(1), last_offsets, lambda: quantize_w(2)),
+              (lambda: two_offsets(2), last_scatter),
+              (last_list,),
+              (lambda: quantize_w(4),))
 
     def product(i, bank, a, b, win, name):
         p = 512 * bank
         up(X.matmul_mx(T.psy[:, p:p + b - a], T.wqc[:, 128 * i:128 * i + 128], T.wqs[:, 128 * i:128 * i + 128], win[0][:, a:b], win[1][:, a:b], True, True), name)
+
+    def copy_out(on, t, o):
+        i = O * t + o
+        out, in_ = T.ysb[:, K * i:K * i + K], T.psy[:, 512 * (i % 6):512 * (i % 6) + K]
+        wait(on, "y%s%d" % ("mn"[o], t))
+        up(V.tensor_copy(out, in_) if on is V else S.activation(out, in_, AF.Copy), "ev%d" % t)
+
+    BETWEEN = (((load_last, 0), (load_w, 2), (load_w, 3)), ((spread, 2), (spread, 3)), ((store_y, 0),),
+               ((load_w, 4), (store_y, 1)), ((store_y, 2), (store_y, 3)))
+
+    def between(t):
+        wait(Y, "snt%d" % t)
+        if t == 1:
+            wait(Y, "lqr")
+        for move, i in BETWEEN[t]:
+            move(i)
 
     between(0)
     OLD, END, NEW = 2, 3, 4
 
     for t in range(R):
         last = t + 1 == R
-        two = 0 < t < R - 1
         wc, ws = T["winc%d" % t], T["wins%d" % t]
+        ix = IX * t
         if t == 0:
             wait(X, "uq")
             wait(X, "xq")
+        if t in EARLY:
+            both("arp%d" % t)
+            for c in range(2):
+                v(V.tensor_scalar(T.offg[:, 2 * t + c:2 * t + c + 1], T["goti%d" % t][:, c:c + 1], float(B), T.less[:, c:c + 1], AL.mult, AL.subtract), "got%d" % t)
+            both("got%d" % t)
+            at = slice(B * others.index(giver), B * others.index(giver) + B)
+            pick(wc[:, at], ws[:, at], T["gotc%d" % t][:, :], T["gots%d" % t][:, :], T.offg[:, 2 * t:2 * t + 2], ("got%d" % t,) * 2)
+            both("got%d" % t)
+            wait(X, "got%d" % t)
         wait(X, "arr%d" % t)
         bank = 512 * (t % 2)
         up(X.matmul_mx(T.psc[:, bank:bank + 128], T.uqc[:, :], T.uqs[:, :], wc[:, 0:128], ws[:, 0:128], True, True), "sco%d" % t)
-        if two:
+        early = t + 1 in EARLY
+        if not last:
             tc, ts = T["twoc%d" % t], T["twos%d" % t]
-            for name in ("oa%d" % t, "tc%d" % (t - 1), "ts%d" % (t - 1), "arr%d" % t):
+            for name in ["oa%d" % t] + (["tc%d" % (t - 1), "ts%d" % (t - 1)] if t else []) + ["arr%d" % t]:
                 both(name)
-            pick(tc[:, :], ts[:, :], wc[:, :], ws[:, :], T.offa[:, 4 * t:4 * t + 4], ("two%d" % t,) * 2)
+            at = [slice(2 * B * i, 2 * B * i + 2 * B) for i in range(2)]
+            oc = [T.offa[:, PS * t + 4 * i:PS * t + 4 * i + 4] for i in range(2)]
+            if early:
+                form_early(t, 1, wc[:, :], ws[:, :])
+            else:
+                up(S.activation(ts[:, at[0]], ws[:, :].indirect(oc[0]), AF.Copy), "two%d" % t)
+            for i in range(early, 2):
+                v(V.tensor_copy(tc[:, at[i]].bitcast(dt.uint32), wc[:, :].bitcast(dt.uint32).indirect(oc[i])))
         wait(S, "sco%d" % t)
         up(S.activation(T.sg[:, NB * t:NB * t + NB], T.psc[:, bank:bank + NB], AF.Sign, bias=-1e-30, scale=-1.0, accum_out=T.cnt[:, t:t + 1]), "act%d" % t)
+        if not last:
+            up(S.activation(ts[:, at[1]], ws[:, :].indirect(oc[1]), AF.Copy), "two%d" % t)
         if last:
             product(O * t, NEW, 0, 128, (wc, ws), "nm")
             wait(S, "nm")
             up(S.activation(T.yw[:, 0:128], T.psy[:, 512 * NEW:512 * NEW + 128], AF.Copy), "ne")
         vw()
-        if two:
-            both("two%d" % t)
         if not last:
+            wait(S, "two%d" % t)
             wait(V, "lw%d" % t)
         wait(V, "act%d" % t)
-        v(V.tensor_scalar(T.idx[:, 4 * t:4 * t + 3], T.base[:, t:3 * R:R], T.cnt[:, t:t + 1], 1.0 / 512, AL.subtract, AL.mult), "ix%d" % t)
+        v(V.tensor_scalar(T.idx[:, ix:ix + IX - 1], T.base[:, t:(IX - 1) * R:R], T.cnt[:, t:t + 1], 1.0 / 512, AL.subtract, AL.mult), "ix%d" % t)
         wait(V, "ix%d" % t)
-        if two:
-            wait(S, "ix%d" % t)
-            pick_hop(t + 1, True, tc[:, :], ts[:, :], lambda a, b: T.idx[:, 4 * t:4 * t + 2])
         if not last:
-            v(V.tensor_scalar(T["offs%d" % t][:, :], T.lw[:, t, PW:PE].indirect(T.idx[:, 4 * t + 2:4 * t + 3]), float(LESS), None, AL.add), "ofr%d" % t)
+            wait(S, "ix%d" % t)
+            if early:
+                send_early(t + 1, "ix%d" % t, T.idx[:, ix:ix + 2], T["goti%d" % (t + 1)][:, :])
+            for role in range(early, 2):
+                pick_hop(t + 1, role, tc[:, at[role]], ts[:, at[role]], T.idx[:, ix:ix + 2])
+            v(V.tensor_scalar(T["offs%d" % t][:, :], T.lw[:, t, PS:PS + 2 * GS].indirect(T.idx[:, ix + 2:ix + 3]), float(NB), None, AL.add), "ofr%d" % t)
+        pairs = T.lq[:, PT:PE] if last else T.lw[:, t, PT:PE]
+        v(V.tensor_scalar(T.offt[:, 16 * t:16 * t + 16], pairs.indirect(T.idx[:, ix + 4:ix + 5]), float(NB), None, AL.add), "ew%d" % t)
+        if not last:
             both("ofr%d" % t)
-            for first in (False,) if two else (True, False):
-                pick_hop(t + 1, first, wc[:, :], ws[:, :], lambda a, b: T["offs%d" % t][:, a:b])
+            d = roles(r)[2]
+            pick_hop(t + 1, 2, wc[:, :], ws[:, :], T["offs%d" % t][:, 2 * d:2 * d + 2])
             send(t + 1)
-        pairs = T.lq[:, 0:PW] if last else T.lw[:, t, 0:PW]
-        v(V.tensor_scalar(T.offt[:, 16 * t:16 * t + 16], pairs.indirect(T.idx[:, 4 * t:4 * t + 1]), float(LESS), None, AL.add), "ew%d" % t)
         both("ew%d" % t)
         if last:
             break
         nc, ns = T["winc%d" % (t + 1)], T["wins%d" % (t + 1)]
         pick(nc[:, NB:WIN], ns[:, NB:WIN], wc[:, :], ws[:, :], T.offt[:, 16 * t:16 * t + KC], ("tc%d" % t, "ts%d" % t))
         if t == 0:
-            two_lists()
-        if t + 2 < R:
-            spread(t + 1, 0)
+            spread(1)
+        else:
+            for o in range(O):
+                copy_out(S, t - 1, o)
         for work in BEHIND[t]:
             work()
         wait(X, "tc%d" % t)
@@ -359,20 +429,18 @@ def rank_program(g, core, T, topo):
         wait(X, "wq%d" % t)
         if t >= 3:
             wait(X, "ev%d" % (t - 3))
-        for o, name in enumerate(("ym%d" % t, "yn%d" % t)):
+        for o in range(O):
             i = O * t + o
-            product(i, i % 6, NB, WIN, (nc, ns), name)
-            out, in_ = T.ysb[:, K * i:K * i + K], T.psy[:, 512 * (i % 6):512 * (i % 6) + K]
-            on = V if o and t in SHARED else S
-            wait(on, name)
-            up(V.tensor_copy(out, in_) if on is V else S.activation(out, in_, AF.Copy), "ev%d" % t)
+            product(i, i % 6, NB, WIN, (nc, ns), "y%s%d" % ("mn"[o], t))
         if t == R - 2:
+            copy_out(S, t, 0)
+            copy_out(V, t, 1)
             wait(X, "wq%d" % (t + 1))
             wait(X, "ev1")
             wait(X, "ev2")
             product(O * (t + 1), OLD, 128, WIN, (nc, ns), "om")
-            wait(S, "om")
-            up(S.activation(T.yw[:, 128:WIN], T.psy[:, 512 * OLD:512 * OLD + WIN - 128], AF.Copy), "oe")
+            wait(V, "om")
+            v(V.tensor_copy(T.yw[:, 128:WIN], T.psy[:, 512 * OLD:512 * OLD + WIN - 128]), "oe")
         between(t + 1)
 
     t = R - 1
@@ -380,20 +448,28 @@ def rank_program(g, core, T, topo):
     part = [slice(K * O * t + HK * i, K * O * t + HK * (i + 1)) for i in range(4)]
     both("oe")
     both("ne")
-    v(V.tensor_copy(T.ysb[:, part[0]], T.yw[:, :].indirect(half[0])), "lp")
-    up(S.activation(T.ysb[:, part[1]], T.yw[:, :].indirect(half[1]), AF.Copy), "lp")
+
+    def results(h, name):
+        for i in range(2):
+            c, e = part[h].start + HK // 2 * i, 16 * t + KC // 4 * (2 * h + i)
+            out, in_ = T.ysb[:, c:c + HK // 2], T.yw[:, :].indirect(T.offt[:, e:e + KC // 4])
+            up(S.activation(out, in_, AF.Copy) if i else V.tensor_copy(out, in_), name)
+
+    results(0, "lp0")
     for h in range(2):
         at = slice(HK * h, HK * h + HK)
         pick(T.endc[:, at], T.ends[:, at], wc[:, :], ws[:, :], half[h], ("lc%d" % h,) * 2)
         wait(X, "lc%d" % h)
         product(O * t + 1, END + 2 * h, HK * h, HK * h + HK, (T.endc, T.ends), "lm%d" % h)
+    results(1, "le0")
     wait(V, "lm0")
     v(V.tensor_copy(T.ysb[:, part[2]], T.psy[:, 512 * END:512 * END + HK]), "le0")
     wait(S, "lm1")
     up(S.activation(T.ysb[:, part[3]], T.psy[:, 512 * (END + 2):512 * (END + 2) + HK], AF.Copy), "le1")
-    for on, ready, at, done in ((Y, "lp", slice(part[0].start, part[1].stop), "yl"), (Y, "le0", part[2], "yl"), (S, "le1", part[3], "kq")):
+    for on, ready, at, done in ((Y, "lp0", part[0], "yl"), (Y, "le0", slice(part[1].start, part[2].stop), "yl"), (S, "le1", part[3], "kq")):
         wait(on, ready)
         up(on.dma_start(T.y[:, at], T.ysb[:, at]), done, 16)
-    for name in total:
+    wait(S, "kq")
+    for name in sorted(total, key=lambda name: name == "yl"):
         if waited.get(name, 0) < total[name]:
             wait(Y, name)

from concourse.bass import DstId, RemoteDMATransfer
from concourse.mybir import dt, AluOpType, ActivationFunctionType

N, K, B, R, O = 4, 256, 32, 5, 2
NB = (N - 1) * B
LC = NB // 16
RC = 2 * N
KC = K // 16
TS, GS = KC + 2, RC + 2
TW, GW = 16 * TS, 16 * GS
HK = K // 2
WIN = NB + K
PS, PT = 8, 32
PE = PT + 2 * TS
IX = 6
EARLY = (2, 3)
TURN = 256.0 + NB + 1

SCRATCH = {
    "psc": ("psum", [128, 1024], "float32"),
    "psy": ("psum", [128, 3072], "float32"),
    "lw": ("sbuf", [128, R - 1, PE + 4], "float32"),
    "lz": ("sbuf", [128, PS, 32], "bfloat16"), "tz": ("sbuf", [128, PS, 32], "bfloat16"),
}
for _n, _w, _d in (
        ("xt", 4 * K, "bfloat16"), ("ut", 16, "bfloat16"), ("ur", 512, "bfloat16"), ("zt", 128, "bfloat16"),
        ("uqc", 128, "float8_e4m3fn_x4"), ("uqs", 128, "uint8"),
        ("wt", 512 * R * O, "bfloat16"), ("wqc", 128 * R * O, "float8_e4m3fn_x4"), ("wqs", 128 * R * O, "uint8"),
        ("ci", RC, "int32"), ("cqd", RC, "int32"), ("cqs", GS, "int32"), ("cqe", RC, "int32"),
        ("of0", RC, "uint16"), ("bq", LC + GS, "uint16"), ("be", LC, "uint16"), ("thr1", 16, "int32"), ("thb", 16, "int32"),
        ("pidx", TS, "int32"), ("p15", 1, "int32"), ("p31", TS, "int32"), ("kslot", TS, "int32"), ("oddi", 1, "int32"),
        ("odd16", 1, "float32"), ("even16", 1, "float32"), ("slots", 32, "float32"), ("slot", 32, "float32"),
        ("pe0", 1, "float32"), ("pe1", 1, "float32"), ("pe2", 1, "float32"), ("base", (IX - 1) * R, "float32"),
        ("count", TW + NB - 16, "bfloat16"), ("la", TW, "bfloat16"), ("ta", TW, "bfloat16"), ("lb", TW, "bfloat16"), ("tb", TW, "bfloat16"),
        ("lg", 2 * GW, "bfloat16"), ("tg", 2 * GW, "bfloat16"), ("lq", PE, "float32"),
        ("idx", IX * R, "uint16"), ("offt", 16 * R, "uint16"), ("offa", PS * R, "uint16"),
        ("offe", 32 * R, "uint16"), ("offg", 2 * R, "uint16"), ("forms", 4, "uint16"), ("less", 2, "float32"),
        ("sg", R * NB, "float32"), ("cnt", R, "float32"), ("ysb", R * O * K, "float32"),
        ("yw", WIN, "float32"), ("endc", K, "float8_e4m3fn_x4"), ("ends", K, "uint8")):
    SCRATCH[_n] = ("sbuf", [128, _w], _d)
for _t in range(R):
    SCRATCH["sndc%d" % _t] = ("sbuf", [128, N * B], "float8_e4m3fn_x4")
    SCRATCH["snds%d" % _t] = ("sbuf", [128, N * B], "uint8")
    SCRATCH["offs%d" % _t] = ("sbuf", [128, 16], "uint16")
    SCRATCH["twoc%d" % _t] = ("sbuf", [128, 4 * B], "float8_e4m3fn_x4")
    SCRATCH["twos%d" % _t] = ("sbuf", [128, 4 * B], "uint8")
    SCRATCH["winc%d" % _t] = ("sbuf", [128, WIN], "float8_e4m3fn_x4")
    SCRATCH["wins%d" % _t] = ("sbuf", [128, WIN], "uint8")

SEMAPHORES = ["xl", "csl", "cdl", "cql", "cel", "ul", "iot", "iok", "ioc", "ios", "con", "pad", "fla", "flb", "tbc", "ztr", "urr", "uq",
              "xq", "o0", "vq", "kq", "yl", "bqr", "sca", "gu", "gc", "lqr", "lzr", "om", "oe", "nm", "ne"]
for _t in range(R):
    SEMAPHORES += ["%s%d" % (n, _t) for n in ("arr", "snt", "pc0", "pc1", "pc2", "ps0", "ps1", "ps2", "ix", "sco", "act", "wl", "wq", "ew")]
    SEMAPHORES += ["%s%d" % (n, _t) for n in ("two", "oa", "tc", "ts", "ofr", "ym", "yn", "ev", "lw") if _t < R - 1]
SEMAPHORES += ["%s%d" % (n, o) for n in ("lm", "le", "lc") for o in range(2)] + ["lp0"]
for _t in EARLY:
    SCRATCH["gotc%d" % _t] = ("sbuf", [128, 2 * B], "float8_e4m3fn_x4")
    SCRATCH["gots%d" % _t] = ("sbuf", [128, 2 * B], "uint8")
    SCRATCH["goti%d" % _t] = ("sbuf", [128, 2], "uint16")
    SEMAPHORES += ["arp%d" % _t, "got%d" % _t]

AL = AluOpType
AF = ActivationFunctionType


def rank_program(g, core, T, topo):
    r = T.rank_of(core)
    if r is None:
        return
    others = [s for s in range(N) if s != r]
    V, S, X, Y = g.vector, g.scalar, g.tensor, g.sync
    total = {}
    waited = {}

    def up(call, name, n=1):
        call.then_inc(T.sem[name], n)
        total[name] = total.get(name, 0) + n

    def wait(q, name):
        q.wait_ge(T.sem[name], total[name])
        waited[name] = total[name]

    def v(call, name="vq"):
        up(call, name)

    def vw():
        wait(V, "vq")

    def both(name):
        wait(V, name)
        wait(S, name)

    def load_w(t):
        up(Y.dma_start(T.wt[:, 1024 * t:1024 * t + 1024], T.w[:, 1024 * t:1024 * t + 1024]), "wl%d" % t, 16)

    def store_y(t):
        wait(Y, "ev%d" % t)
        up(Y.dma_start(T.y[:, O * K * t:O * K * (t + 1)], T.ysb[:, O * K * t:O * K * (t + 1)]), "yl", 16)

    def load_list(on, out, a, keys, t, name):
        up(on.dma_start(out, keys[:, RC * t:RC * (t + 1)]), name, 16)

    def load_last(_):
        for a in range(8):
            load_list(Y, T.cqe[16 * a:16 * a + 16, :], a, T.cd, R - 1, "cel")

    v(V.memset(T.cqs[:, :], 0), "pad")
    for a in range(2):
        load_list(S if a else Y, T.ci[16 * a:16 * a + 16, :], a, T.cs, 0, "csl")
    up(Y.dma_start(T.xt[:, :], T.x[:, :]), "xl", 16)
    up(Y.dma_start(T.ut[:, :], T.u[:, 0:16]), "ul", 16)
    up(Y.dma_start(T.thr1[0:1, :], T.thr[:, :]), "ul", 16)
    wait(Y, "pad")
    for a in range(8):
        load_list(S, T.cqd[16 * a:16 * a + 16, :], a, T.cd, a // 2, "cdl")
        load_list(Y, T.cqs[16 * a:16 * a + 16, a % 2:a % 2 + RC], a, T.cs, a // 2 + 1, "cql")
    load_w(0)
    load_w(1)

    up(g.iota(T.pidx[:, :], [[0, TS]], 0, 1), "iot")
    up(g.iota(T.kslot[:, :], [[32, TS // 2], [-16, 2]], 0, 0), "iok")
    up(g.iota(T.count[:, :], [[1, TW + NB - 16]], -NB, 0, allow_small_or_imprecise_dtypes=True), "ioc")

    v(V.memset(T.zt[:, :], 0.0), "ztr")
    v(V.memset(T.lq[:, PS + 2 * GS:PT], 0.0))
    wait(V, "iot")
    v(V.tensor_scalar(T.oddi[:, :], T.pidx[:, 0:1], 16, None, AL.bitwise_and))
    v(V.tensor_scalar(T.p31[:, :], T.pidx[:, :], 31, None, AL.bitwise_and))
    vw()
    v(V.tensor_scalar(T.even16[:, :], T.oddi[:, :], -1.0, 16.0, AL.mult, AL.add), "con")
    v(V.tensor_copy(T.odd16[:, :], T.oddi[:, :]))
    wait(S, "ioc")
    wait(S, "con")
    for table, name in ((T.lb, "flb"), (T.la, "fla")):
        up(S.activation(table[:, :], T.count[:, NB - 16:], AF.Identity, bias=T.even16[:, 0:1]), name)

    def roles(s):
        rest = [d for d in range(N) if d != s]
        return sorted(rest, key=lambda d: (topo.same_plane(topo.chip(T.cores[s]), topo.chip(T.cores[d])), d == rest[1], abs(d - s)))

    runs = []
    if r > 0:
        runs.append((0, 0, 2 * r))
    if r < N - 1:
        runs.append((2 * r + 2, 2 * r, LC - 2 * r))
    q = [slice(32 * k, 32 * k + 32) for k in range(4)]
    giver = [s for s in others if roles(s)[0] == r][0]

    wait(V, "csl")
    for k in range(4):
        v(V.tensor_copy(T.of0[q[k], :], T.ci[q[0], :]), "o0")
    wait(V, "xl")
    v(V.quantize_mx(T.winc0[:, NB:WIN], T.wins0[:, NB:WIN], T.xt[:, :]), "xq")

    def pick(codes, scales, wc, ws, oc, names):
        v(V.tensor_copy(codes.bitcast(dt.uint32), wc.bitcast(dt.uint32).indirect(oc)), names[0])
        up(S.activation(scales, ws.indirect(oc), AF.Copy), names[1])

    def pick_hop(t, role, wc, ws, oc):
        at = slice(B * roles(r)[role], B * roles(r)[role] + B)
        pick(T["sndc%d" % t][:, at], T["snds%d" % t][:, at], wc, ws, oc, ["p%s%d%d" % (n, role, t) for n in "cs"])

    both("o0")
    both("xq")
    for role, d in enumerate(roles(r)):
        pick_hop(0, role, T.winc0[:, NB:WIN], T.wins0[:, NB:WIN], T.of0[:, 2 * d:2 * d + 2])

    PLAN = [[("c", 0, 0, 1)], [("c", 1, 0, 1)], [("s", 0, 0, 2), ("s", 1, 1, 2)], [("c", 2, 0, 1)], [("s", 2, 0, 1)]]
    FIRST = [[("c", 0, 0, 2)], [("c", 1, 1, 2)]] + PLAN[2:]
    LATE = [[(kind, role, 0, 1)] for role in (1, 2) for kind in "cs"]

    def engines(s, role, first, step):
        return topo.engines(T.cores[s], T.cores[roles(s)[role]])[first::step]

    def piece(t, kind, role, first, step):
        wait(g, "p%s%d%d" % (kind, role, t))
        d = roles(r)[role]
        rid, pid, _ = topo.addr(T.cores[d])
        at = B * (r if r < d else r - 1)
        src = T["snd%s%d" % (kind, t)][:, B * d:B * d + B]
        dst = T["win%s%d" % (kind, t)][:, at:at + B]
        if kind == "c":
            src, dst = src.bitcast(dt.uint8), dst.bitcast(dt.uint8)
        return RemoteDMATransfer(dst_ids=[DstId(rid=rid, pnc=pid)], dma_engine_mask=sum(1 << e for e in engines(r, role, first, step)),
                                 remote_sem=T.sem["arr%d" % t], srcs=[src], dsts=[dst])

    def send_early(t, ready, src, dst):
        wait(g, ready)
        rid, pid, _ = topo.addr(T.cores[roles(r)[0]])
        g.remote_dma(dst, src, T.sem["arp%d" % t], T.sem["snt%d" % t], pid, rid, topo.mask(core, T.cores[roles(r)[0]]))
        total["snt%d" % t] = total.get("snt%d" % t, 0) + len(engines(r, 0, 0, 1))
        total["arp%d" % t] = total.get("arp%d" % t, 0) + len(engines(giver, 0, 0, 1))

    def send(t):
        plan = []
        for call in LATE if t in EARLY else PLAN if t else FIRST:
            g.remote_dma_fused([piece(t, *p) for p in call], local_sem=T.sem["snt%d" % t])
            plan += call
        total["snt%d" % t] = total.get("snt%d" % t, 0) + sum(len(engines(r, *p[1:])) for p in plan)
        total["arr%d" % t] = sum(len(engines(s, *p[1:])) for s in others for p in plan if roles(s)[p[1]] == r)

    send(0)

    for o, (step, first) in enumerate(((3, 0), (-1, 1))):
        up(g.iota(T.slots[:, 16 * o:16 * o + 16], [[2048, 8], [1024 * step, 2]], int(TURN) + 1024 * first, 0, allow_small_or_imprecise_dtypes=True), "ios")
    wait(g, "ul")
    up(g.partition_broadcast(T.thb[:, :], T.thr1[0:1, :], 128), "tbc")

    def repeat_u(i):
        up(S.activation(T.ur[:, i:512:4], T.zt[:, :], AF.Identity, bias=T.ut[:, i:i + 1]), "urr")

    def interleave(c):
        for i, d in enumerate(roles(r)[:2]):
            for h in range(2):
                up(S.activation(T.lz[:, 4 * i:4 * i + 4, 16 * h + c:16 * h + 16:2], T.lg[:, GW * c + B * d:GW * c + B * d + B], AF.Copy), "lzr")

    vw()
    wait(V, "cql")
    v(V.tensor_scalar(T.bq[:, LC:], T.cqs[:, :], T.odd16[:, 0:1], None, AL.add), "bqr")
    wait(V, "cdl")
    for a, b, n in runs:
        v(V.tensor_scalar(T.bq[:, b:b + n], T.cqd[:, a:a + n], T.odd16[:, 0:1], None, AL.add))
    wait(V, "fla")
    vw()
    v(V.tensor_copy(T.la[:, :].indirect(T.bq[:, 0:LC]), T.count[:, 0:NB]), "sca")
    wait(S, "ul")
    wait(S, "ztr")
    repeat_u(0)
    for c, (table, ready, name) in enumerate(((T.lb, ("flb", "bqr"), "gu"), (T.la, ("sca",), "gc"))):
        for n in ready:
            wait(S, n)
        up(S.activation(T.lg[:, GW * c:GW * c + GW], table[:, :].indirect(T.bq[:, LC:]), AF.Copy), name)
        wait(S, name)
        interleave(c)
    for i in range(1, 4):
        repeat_u(i)
    wait(V, "sca")
    v(V.transpose(T.ta[:, :], T.la[:, :]))
    wait(V, "iok")
    v(V.tensor_tensor(T.lq[:, PT:PE:2], T.p31[:, :], T.kslot[:, :], AL.add), "lqr")
    v(V.tensor_scalar(T.p15[:, :], T.pidx[:, 0:1], 15, None, AL.bitwise_and))
    vw()
    v(V.tensor_copy(T.lq[:, PT + 1:PE:2], T.ta[:, 0:TW:16]), "lqr")
    v(V.tensor_scalar(T.pe0[:, :], T.p15[:, :], 1024.0, TURN, AL.mult, AL.add))
    v(V.tensor_scalar(T.pe1[:, :], T.p15[:, :], 1024.0, TURN + 16 * 1024, AL.mult, AL.add))
    wait(V, "gu")
    wait(V, "gc")
    v(V.transpose(T.tg[:, :], T.lg[:, :]))
    wait(V, "lzr")
    v(V.transpose(T.tz[:, :, :], T.lz[:, :, :]))
    vw()
    for c in range(2):
        v(V.tensor_copy(T.lq[:, PS + c:PS + 2 * GS:2], T.tg[:, GW * c:GW * c + GW:16]), "lqr")
    v(V.tensor_copy(T.lq[:, 0:PS], T.tz[:, :, 0]), "lqr")
    for k in range(4):
        v(V.tensor_scalar(T.offa[q[k], 0:PS], T.tz[q[0], :, 0], float(NB), None, AL.add), "oa0")

    def two_offsets(t):
        wait(V, "lw%d" % t)
        v(V.tensor_scalar(T.offa[:, PS * t:PS * t + PS], T.lw[:, t, 0:PS], float(NB), None, AL.add), "oa%d" % t)
        if t + 1 in EARLY:
            for c in range(2):
                v(V.tensor_scalar(T.offe[:, 32 * t + 16 * c:32 * t + 16 * c + 16], T.lw[:, t, PS:PS + 2 * GS].indirect(T.forms[:, 2 * c:2 * c + 1]),
                                  float(NB * c), None, AL.add), "oa%d" % t)
            for name in ("oa%d" % t, "tc%d" % (t - 1), "ts%d" % (t - 1)):
                both(name)
            form_early(t, 0, T["winc%d" % t][:, NB:WIN], T["wins%d" % t][:, NB:WIN])

    def form_early(t, c, wc, ws):
        at, e = slice(B * c, B * c + B), 32 * t + 16 * c + 2 * roles(r)[0]
        tc, ts = T["twoc%d" % t][:, at], T["twos%d" % t][:, at]
        pick(tc, ts, wc, ws, T.offe[:, e:e + 2], ("pc0%d" % (t + 1), "ps0%d" % (t + 1)))
        send_early(t + 1, "pc0%d" % (t + 1), tc.bitcast(dt.uint8), T["gotc%d" % (t + 1)][:, at].bitcast(dt.uint8))
        send_early(t + 1, "ps0%d" % (t + 1), ts, T["gots%d" % (t + 1)][:, at])

    def spread(t):
        for k in range(4):
            out, in_ = T.lw[q[k], t, 0:PE], T.lq[q[t], :]
            if t < 2:
                up(S.activation(out, in_, AF.Copy), "lw%d" % t)
            else:
                up(Y.dma_start(out, in_), "lw%d" % t, 16)

    wait(V, "urr")
    v(V.quantize_mx(T.uqc[:, :], T.uqs[:, :], T.ur[:, :]), "uq")
    wait(S, "lqr")
    spread(0)
    wait(V, "ios")
    v(V.transpose(T.slot[:, :], T.slots[:, :]))
    wait(V, "tbc")
    v(V.tensor_scalar(T.base[:, 0:R], T.thb[:, 0:R], -2.0, T.pe0[:, 0:1], AL.mult, AL.add))
    v(V.tensor_scalar(T.base[:, R:2 * R], T.thb[:, 0:R], -2.0, T.pe1[:, 0:1], AL.mult, AL.add))
    vw()
    v(V.tensor_scalar(T.pe2[:, :], T.slot[:, 0:1], 1024.0 * (GS - 1) + TURN, None, AL.min))
    v(V.tensor_scalar(T.base[:, 4 * R:5 * R], T.thb[:, 0:R], -2.0, T.slot[:, 0:1], AL.mult, AL.add))
    vw()
    v(V.tensor_scalar(T.base[:, 2 * R:4 * R], T.thb[:, 0:2 * R], -2.0, T.pe2[:, 0:1], AL.mult, AL.add))

    def early_constants():
        for c in range(2):
            v(V.tensor_scalar(T.forms[:, 2 * c:2 * c + 1], T.pe2[:, :], 512.0 * c - TURN, 1.0 / 512, AL.add, AL.mult))
            v(V.tensor_scalar(T.less[:, c:c + 1], T.p15[:, :], 63.0, 63.0 * 16 * c, AL.mult, AL.add))
        vw()

    def quantize_w(t):
        wait(V, "wl%d" % t)
        for i in (2 * t, 2 * t + 1):
            v(V.quantize_mx(T.wqc[:, 128 * i:128 * i + 128], T.wqs[:, 128 * i:128 * i + 128], T.wt[:, 512 * i:512 * i + 512]), "wq%d" % t)

    def last_offsets():
        wait(V, "cel")
        for a, b, n in runs:
            v(V.tensor_scalar(T.be[:, b:b + n], T.cqe[:, a:a + n], T.odd16[:, 0:1], None, AL.add))

    def last_scatter():
        v(V.tensor_copy(T.lb[:, :].indirect(T.be[:, :]), T.count[:, 0:NB]))

    def last_list():
        v(V.transpose(T.tb[:, :], T.lb[:, :]))
        two_offsets(R - 2)
        quantize_w(R - 2)
        vw()
        v(V.tensor_copy(T.lq[:, PT + 1:PE:2], T.tb[:, 0:TW:16]))

    quantize_w(0)
    BEHIND = ((early_constants, lambda: two_offsets(1), lambda: quantize_w(1), last_offsets, lambda: quantize_w(2)),
              (lambda: two_offsets(2), last_scatter),
              (last_list,),
              (lambda: quantize_w(4),))

    def product(i, bank, a, b, win, name):
        p = 512 * bank
        up(X.matmul_mx(T.psy[:, p:p + b - a], T.wqc[:, 128 * i:128 * i + 128], T.wqs[:, 128 * i:128 * i + 128], win[0][:, a:b], win[1][:, a:b], True, True), name)

    def copy_out(on, t, o):
        i = O * t + o
        out, in_ = T.ysb[:, K * i:K * i + K], T.psy[:, 512 * (i % 6):512 * (i % 6) + K]
        wait(on, "y%s%d" % ("mn"[o], t))
        up(V.tensor_copy(out, in_) if on is V else S.activation(out, in_, AF.Copy), "ev%d" % t)

    BETWEEN = (((load_last, 0), (load_w, 2), (load_w, 3)), ((spread, 2), (spread, 3)), ((store_y, 0),),
               ((load_w, 4), (store_y, 1)), ((store_y, 2), (store_y, 3)))

    def between(t):
        wait(Y, "snt%d" % t)
        if t == 1:
            wait(Y, "lqr")
        for move, i in BETWEEN[t]:
            move(i)

    between(0)
    OLD, END, NEW = 2, 3, 4

    for t in range(R):
        last = t + 1 == R
        wc, ws = T["winc%d" % t], T["wins%d" % t]
        ix = IX * t
        if t == 0:
            wait(X, "uq")
            wait(X, "xq")
        if t in EARLY:
            both("arp%d" % t)
            for c in range(2):
                v(V.tensor_scalar(T.offg[:, 2 * t + c:2 * t + c + 1], T["goti%d" % t][:, c:c + 1], float(B), T.less[:, c:c + 1], AL.mult, AL.subtract), "got%d" % t)
            both("got%d" % t)
            at = slice(B * others.index(giver), B * others.index(giver) + B)
            pick(wc[:, at], ws[:, at], T["gotc%d" % t][:, :], T["gots%d" % t][:, :], T.offg[:, 2 * t:2 * t + 2], ("got%d" % t,) * 2)
            both("got%d" % t)
            wait(X, "got%d" % t)
        wait(X, "arr%d" % t)
        bank = 512 * (t % 2)
        up(X.matmul_mx(T.psc[:, bank:bank + 128], T.uqc[:, :], T.uqs[:, :], wc[:, 0:128], ws[:, 0:128], True, True), "sco%d" % t)
        early = t + 1 in EARLY
        if not last:
            tc, ts = T["twoc%d" % t], T["twos%d" % t]
            for name in ["oa%d" % t] + (["tc%d" % (t - 1), "ts%d" % (t - 1)] if t else []) + ["arr%d" % t]:
                both(name)
            at = [slice(2 * B * i, 2 * B * i + 2 * B) for i in range(2)]
            oc = [T.offa[:, PS * t + 4 * i:PS * t + 4 * i + 4] for i in range(2)]
            if early:
                form_early(t, 1, wc[:, :], ws[:, :])
            else:
                up(S.activation(ts[:, at[0]], ws[:, :].indirect(oc[0]), AF.Copy), "two%d" % t)
            for i in range(early, 2):
                v(V.tensor_copy(tc[:, at[i]].bitcast(dt.uint32), wc[:, :].bitcast(dt.uint32).indirect(oc[i])))
        wait(S, "sco%d" % t)
        up(S.activation(T.sg[:, NB * t:NB * t + NB], T.psc[:, bank:bank + NB], AF.Sign, bias=-1e-30, scale=-1.0, accum_out=T.cnt[:, t:t + 1]), "act%d" % t)
        if not last:
            up(S.activation(ts[:, at[1]], ws[:, :].indirect(oc[1]), AF.Copy), "two%d" % t)
        if last:
            product(O * t, NEW, 0, 128, (wc, ws), "nm")
            wait(S, "nm")
            up(S.activation(T.yw[:, 0:128], T.psy[:, 512 * NEW:512 * NEW + 128], AF.Copy), "ne")
        vw()
        if not last:
            wait(S, "two%d" % t)
            wait(V, "lw%d" % t)
        wait(V, "act%d" % t)
        v(V.tensor_scalar(T.idx[:, ix:ix + IX - 1], T.base[:, t:(IX - 1) * R:R], T.cnt[:, t:t + 1], 1.0 / 512, AL.subtract, AL.mult), "ix%d" % t)
        wait(V, "ix%d" % t)
        if not last:
            wait(S, "ix%d" % t)
            if early:
                send_early(t + 1, "ix%d" % t, T.idx[:, ix:ix + 2], T["goti%d" % (t + 1)][:, :])
            for role in range(early, 2):
                pick_hop(t + 1, role, tc[:, at[role]], ts[:, at[role]], T.idx[:, ix:ix + 2])
            v(V.tensor_scalar(T["offs%d" % t][:, :], T.lw[:, t, PS:PS + 2 * GS].indirect(T.idx[:, ix + 2:ix + 3]), float(NB), None, AL.add), "ofr%d" % t)
        pairs = T.lq[:, PT:PE] if last else T.lw[:, t, PT:PE]
        v(V.tensor_scalar(T.offt[:, 16 * t:16 * t + 16], pairs.indirect(T.idx[:, ix + 4:ix + 5]), float(NB), None, AL.add), "ew%d" % t)
        if not last:
            both("ofr%d" % t)
            d = roles(r)[2]
            pick_hop(t + 1, 2, wc[:, :], ws[:, :], T["offs%d" % t][:, 2 * d:2 * d + 2])
            send(t + 1)
        both("ew%d" % t)
        if last:
            break
        nc, ns = T["winc%d" % (t + 1)], T["wins%d" % (t + 1)]
        pick(nc[:, NB:WIN], ns[:, NB:WIN], wc[:, :], ws[:, :], T.offt[:, 16 * t:16 * t + KC], ("tc%d" % t, "ts%d" % t))
        if t == 0:
            spread(1)
        else:
            for o in range(O):
                copy_out(S, t - 1, o)
        for work in BEHIND[t]:
            work()
        wait(X, "tc%d" % t)
        wait(X, "ts%d" % t)
        wait(X, "wq%d" % t)
        if t >= 3:
            wait(X, "ev%d" % (t - 3))
        for o in range(O):
            i = O * t + o
            product(i, i % 6, NB, WIN, (nc, ns), "y%s%d" % ("mn"[o], t))
        if t == R - 2:
            copy_out(S, t, 0)
            copy_out(V, t, 1)
            wait(X, "wq%d" % (t + 1))
            wait(X, "ev1")
            wait(X, "ev2")
            product(O * (t + 1), OLD, 128, WIN, (nc, ns), "om")
            wait(V, "om")
            v(V.tensor_copy(T.yw[:, 128:WIN], T.psy[:, 512 * OLD:512 * OLD + WIN - 128]), "oe")
        between(t + 1)

    t = R - 1
    half = [T.offt[:, 16 * t + KC // 2 * h:16 * t + KC // 2 * (h + 1)] for h in range(2)]
    part = [slice(K * O * t + HK * i, K * O * t + HK * (i + 1)) for i in range(4)]
    both("oe")
    both("ne")

    def results(h, name):
        for i in range(2):
            c, e = part[h].start + HK // 2 * i, 16 * t + KC // 4 * (2 * h + i)
            out, in_ = T.ysb[:, c:c + HK // 2], T.yw[:, :].indirect(T.offt[:, e:e + KC // 4])
            up(S.activation(out, in_, AF.Copy) if i else V.tensor_copy(out, in_), name)

    results(0, "lp0")
    for h in range(2):
        at = slice(HK * h, HK * h + HK)
        pick(T.endc[:, at], T.ends[:, at], wc[:, :], ws[:, :], half[h], ("lc%d" % h,) * 2)
        wait(X, "lc%d" % h)
        product(O * t + 1, END + 2 * h, HK * h, HK * h + HK, (T.endc, T.ends), "lm%d" % h)
    results(1, "le0")
    wait(V, "lm0")
    v(V.tensor_copy(T.ysb[:, part[2]], T.psy[:, 512 * END:512 * END + HK]), "le0")
    wait(S, "lm1")
    up(S.activation(T.ysb[:, part[3]], T.psy[:, 512 * (END + 2):512 * (END + 2) + HK], AF.Copy), "le1")
    for on, ready, at, done in ((Y, "lp0", part[0], "yl"), (Y, "le0", slice(part[1].start, part[2].stop), "yl"), (S, "le1", part[3], "kq")):
        wait(on, ready)
        up(on.dma_start(T.y[:, at], T.ysb[:, at]), done, 16)
    wait(S, "kq")
    for name in sorted(total, key=lambda name: name == "yl"):
        if waited.get(name, 0) < total[name]:
            wait(Y, name)
